import numpy as np
import ml_dtypes


def mxq(x, axis, fmt="e4m3"):
    dtype, down = {"e4m3": (ml_dtypes.float8_e4m3fn, 7), "e5m2": (ml_dtypes.float8_e5m2, 14)}[fmt]
    v = np.moveaxis(np.asarray(x, np.float32).astype(ml_dtypes.bfloat16).astype(np.float64), axis, -1)
    blocks = v.reshape(v.shape[:-1] + (-1, 32))
    amax = np.abs(blocks).max(-1, keepdims=True)
    byte = np.maximum(np.where(amax > 0, np.frexp(amax)[1] - 1 + 127, 0) - down, 1)
    scale = np.exp2(byte - 127.0)
    codes = (blocks / scale).astype(np.float32).astype(dtype).astype(np.float64)
    return np.moveaxis((codes * scale).reshape(v.shape), -1, axis)


WIDE = False


def mx_kscale(k):
    if not WIDE:
        return np.ones(k)
    levels = np.array([10, -10, 5, -5, 0])
    if k % 512:
        return np.exp2(np.random.permutation(np.resize(levels, k // 32))).repeat(32)
    a = np.empty((k // 512, 16))
    for p in range(k // 512):
        a[p, :8] = np.random.permutation(np.resize(levels, 8))
        for g in range(8):
            far = levels[np.abs(levels - a[p, g]) >= 10]
            a[p, g + 8] = far[np.random.randint(len(far))]
    return np.exp2(a.ravel()).repeat(32)


def f64(x):
    return np.asarray(x).astype(np.float64)


def striped(idx):
    return np.tile(idx.reshape(-1, 16).T, (8, 1)).astype(np.uint16)


def unstriped(offs):
    return offs[:16].T.reshape(-1).astype(np.int64)


E2M1 = np.array([0.0, 0.5, 1.0, 1.5, 2.0, 3.0, 4.0, 6.0, -0.0, -0.5, -1.0, -1.5, -2.0, -3.0, -4.0, -6.0])


def pack_weight(w, fmt):
    k, n = w.shape
    w = f64(np.asarray(w, np.float32).astype(ml_dtypes.bfloat16)).reshape(k // 32, 32, n)
    amax = np.abs(w).max(1)
    if fmt == "e4m3":
        byte = np.frexp(amax)[1] - 1 + 127 - 7
    else:
        mant, ex = np.frexp(amax / 6.0)
        byte = np.where(mant > 0.5, ex, ex - 1) + 127
    byte = np.clip(np.where(amax > 0, byte, 1), 1, 254)
    scaled = (w * np.exp2(127.0 - byte)[:, None, :]).reshape(k, n).astype(np.float32)
    by_word = np.ascontiguousarray(scaled.reshape(k // 512, 128, 4, n).transpose(0, 1, 3, 2))
    if fmt == "e4m3":
        words = by_word.astype(ml_dtypes.float8_e4m3fn).view(np.uint8)
    else:
        c = by_word.astype(ml_dtypes.float4_e2m1fn).view(np.uint8) & 0xF
        words = (c[..., 0::2] | (c[..., 1::2] << 4)).reshape(k // 512, 128, 2 * n)
    return np.ascontiguousarray(words), np.ascontiguousarray(byte.astype(np.uint8).reshape(k // 512, 16, n))


def unpack_weight(words, scales, fmt):
    g, _, n = scales.shape
    words = np.ascontiguousarray(words).reshape(g, 128, n, -1)
    if fmt == "e4m3":
        vals = words.view(ml_dtypes.float8_e4m3fn).astype(np.float64)
    else:
        nib = np.empty((g, 128, n, 4), np.uint8)
        nib[..., 0::2] = words & 0xF
        nib[..., 1::2] = words >> 4
        vals = E2M1[nib]
    vals = vals * np.repeat(np.exp2(scales.astype(np.float64) - 127.0), 8, axis=1)[..., None]
    return vals.transpose(0, 1, 3, 2).reshape(g * 512, n)


def gelu(v):
    return 0.5 * v * (1.0 + np.tanh(np.sqrt(2.0 / np.pi) * (v + 0.044715 * v**3)))


K, M, H, T, S, T2, P = 512, 1024, 512, 2048, 1024, 2048, 1024

def setup_inputs():
    n = np.random.standard_normal
    s, um, u = mx_kscale(K)[:, None], mx_kscale(M)[:, None], mx_kscale(H)[:, None]
    d = {}
    d["tab_words"], d["tab_scales"] = pack_weight(n((K, T)) * s, "e4m3")
    d["w1"] = (n((K, M)) / s * um.T / K**0.5).astype(np.float32)
    d["w2_words"], d["w2_scales"] = pack_weight(1.5 * n((K, M)) / s / K**0.5, "e2m1")
    d["w3"] = (0.5 * n((M, H)) / um / M**0.5).astype(np.float32)
    d["wgs"] = np.exp(0.3 * n((128, S))).astype(np.float32)
    d["page0"] = np.random.uniform(-1.8, 1.8, (H, T2)).astype(np.float32)
    d["gain"] = (np.exp(0.3 * n(H)) * u[:, 0]).astype(np.float32)
    d["w4_words"], d["w4_scales"] = pack_weight(1.2 * n((H, H)) / u / H**0.5, "e4m3")
    d["base"] = (0.7 * n(H)).astype(np.float32)
    d["offs"] = striped(np.random.permutation(T)[:S])
    d["offs2"] = striped(np.random.permutation(T2)[:S])
    d["offs3"] = striped(np.random.permutation(T2)[:P])
    d["offs4"] = striped(np.random.permutation(T2)[:P])
    return d

def reference(tab_words, tab_scales, w1, w2_words, w2_scales, w3, wgs, page0, gain, w4_words, w4_scales, base, offs, offs2, offs3, offs4):
    v = unpack_weight(tab_words, tab_scales, "e4m3")[:, unstriped(offs)]
    curv = mxq(f64(w1), 0, "e4m3").T @ v
    irr = unpack_weight(w2_words, w2_scales, "e2m1").T @ v
    ratio = curv / (1.0 + np.abs(irr))
    h = mxq(f64(w3), 0, "e4m3").T @ mxq(ratio, 0, "e4m3")
    page = f64(page0).copy()
    page[:, unstriped(offs2)] = np.tile(f64(wgs), (H // 128, 1)) * h
    x = f64(gain)[:, None] * np.sin(page[:, unstriped(offs3)])
    y = unpack_weight(w4_words, w4_scales, "e4m3").T @ mxq(x, 0, "e4m3")
    fellow = page[:, unstriped(offs4)]
    return (y + f64(base)[:, None]) * fellow

@@ -1,0 +1,489 @@
+import math
+from contextlib import ExitStack
+
+import concourse.mybir as mybir
+
+K, M, H, T, S, T2, PN = 512, 1024, 512, 2048, 1024, 2048, 1024
+FLOPS = 2 * (2 * K * M * S + M * H * S + H * H * PN)
+
+F32 = mybir.dt.float32
+BF16 = mybir.dt.bfloat16
+I32 = mybir.dt.int32
+U32 = mybir.dt.uint32
+U16 = mybir.dt.uint16
+U8 = mybir.dt.uint8
+FP8X4 = mybir.dt.float8_e4m3fn_x4
+FP4X4 = mybir.dt.float4_e2m1fn_x4
+ALU = mybir.AluOpType
+ACT = mybir.ActivationFunctionType
+
+P = 128
+CH = 256
+NCH = S // CH
+UW = 128
+HW = 512
+QW = 256
+ROUNDER = 12582912.0
+SMALL_AFTER = 1
+V_RING = 3
+IRR_BANKS = [0,1,2]
+CURV_BANKS = [3,4,6,7]
+EARLY_BANKS = [5]
+LATE_BANKS = [6,7]
+Y_BANKS = [0,1,2,3]
+DAMP_RING = 6
+EARLY_RING = 4
+HAND_RING = 2
+TURN_RING = 2
+REST_RING = 3
+Y_RING = 4
+RES_RING = 4
+CASTS = "vvvv"
+GAIN_ON_VECTOR = ((3, 0), (3, 1))
+WHOLE_RING = 2
+SIN_WARM = 1
+
+
+def tile_list_fellow_eye_fitting_kernel(
+    tc, tab_words, tab_scales, w1, w2_words, w2_scales, w3, wgs, page0, gain,
+    w4_words, w4_scales, base, offs, offs2, offs3, offs4, out,
+):
+    nc = tc.nc
+    with ExitStack() as ctx:
+        lists = ctx.enter_context(tc.tile_pool(name="lists", bufs=1))
+        keep = ctx.enter_context(tc.tile_pool(name="keep", bufs=1))
+        psum = ctx.enter_context(tc.psum_pool(name="psum", bufs=1))
+
+        def kept(name, shape, dtype):
+            return keep.tile(shape, dtype, name=name, align_bytes=64)
+
+        def ring(name, count, shape, dtype):
+            tiles = [kept(f"{name}{i}", shape, dtype) for i in range(count)]
+            turn = []
+
+            def take():
+                turn.append(0)
+                return tiles[(len(turn) - 1) % count]
+
+            return take
+
+        banks = [psum.tile([P, 512], F32, name=f"bank{i}") for i in range(8)]
+
+        def bank_ring(members):
+            turn = []
+
+            def take():
+                turn.append(0)
+                return banks[members[(len(turn) - 1) % len(members)]]
+
+            return take
+
+        def load_list(name, src):
+            tile = lists.tile([P, src.shape[1]], U16, name=name)
+            nc.sync.dma_start(tile[:], src)
+            return tile
+
+        def zeroed_plane(name, width):
+            plane = kept(name, [P, width], U8)
+            nc.vector.memset(plane[:].bitcast(I32), 0)
+            return plane
+
+        def load_plane(plane, src, queue):
+            for quad in range(4):
+                queue.dma_start(
+                    out=plane[32 * quad : 32 * quad + 4, :].bitcast(I32),
+                    in_=src[0, 4 * quad : 4 * quad + 4, :].bitcast(I32),
+                )
+
+        tab_s = zeroed_plane("tab_s", T)
+        w2_s_plane = zeroed_plane("w2_s_plane", M)
+        w4_s_raw = zeroed_plane("w4_s_raw", H)
+
+        list1 = load_list("list1", offs)
+        w2_s_raw = kept("w2_s_raw", [P, M], U8)
+        load_plane(w2_s_raw, w2_scales, nc.scalar)
+        w2_raw = kept("w2_raw", [P, M // 2], I32)
+        nc.sync.dma_start(out=w2_raw[:], in_=w2_words[0].bitcast(I32))
+        tab_w = kept("tab_w", [P, T], I32)
+        nc.sync.dma_start(out=tab_w[:], in_=tab_words[0].rearrange("p t i -> p (t i)").bitcast(I32))
+        load_plane(tab_s, tab_scales, nc.sync)
+        warm = kept("warm", [P, 4], F32)
+        nc.vector.memset(warm[:, 0:1], 1.0)
+        nc.scalar.activation(out=warm[:, 1:2], in_=warm[:, 0:1], func=ACT.Abs_reciprocal_sqrt)
+        w1_raw = [kept(f"w1_raw{b}", [P, 4, 512], F32) for b in range(2)]
+        w3_raw = [kept(f"w3_raw{b}", [P, 4, 512], F32) for b in range(2)]
+        for b in range(2):
+            nc.sync.dma_start(out=w1_raw[b][:], in_=w1[:, 512 * b : 512 * (b + 1)].rearrange("(p j) m -> p j m", j=4))
+        for b in range(2):
+            nc.sync.dma_start(out=w3_raw[b][:], in_=w3[512 * b : 512 * (b + 1), :].rearrange("(p j) r -> p j r", j=4))
+        list2 = load_list("list2", offs2)
+        wgs_rows = wgs.rearrange("(q t) j -> q t j", t=4)
+        wgs_sb = {}
+        page_rows = page0.rearrange("(p t) c -> p t c", t=4)
+        page = [kept(f"page{t}", [P, T2], F32) for t in range(4)]
+
+        def load_wgs(t, half):
+            wgs_sb[t, half] = kept(f"wgs{t}_{half}", [P, S // 2], F32)
+            for quad in range(4):
+                nc.sync.dma_start(
+                    out=wgs_sb[t, half][32 * quad : 32 * (quad + 1)],
+                    in_=wgs_rows[:, t, half * S // 2 : (half + 1) * S // 2],
+                )
+
+        def load_page(t):
+            nc.sync.dma_start(out=page[t][:], in_=page_rows[:, t, :])
+
+        def load_column(name, vec):
+            tile = kept(name, [P, 4], F32)
+            nc.sync.dma_start(out=tile[:], in_=vec.rearrange("(p t) -> p t", t=4))
+            return tile
+
+        def load_w4():
+            raw = kept("w4_raw", [P, H], I32)
+            nc.sync.dma_start(out=raw[:], in_=w4_words[0].rearrange("p c i -> p (c i)").bitcast(I32))
+            load_plane(w4_s_raw, w4_scales, nc.sync)
+            return raw
+
+        for t in range(3):
+            load_wgs(t, 0)
+            load_page(t)
+        load_wgs(0, 1)
+        load_wgs(1, 1)
+        list3 = load_list("list3", offs3)
+        gain_sb = load_column("gain_sb", gain)
+        load_wgs(2, 1)
+        load_wgs(3, 0)
+        load_page(3)
+        load_wgs(3, 1)
+        list4 = load_list("list4", offs4)
+        base_sb = load_column("base_sb", base)
+        w4_raw = load_w4()
+
+        v_w = {}
+        v_s = {}
+        take_v_w = ring("v_w", V_RING, [P, CH], U32)
+        take_v_s = ring("v_s", V_RING, [P, CH], U8)
+
+        def gather_table(c):
+            v_w[c] = take_v_w()
+            v_s[c] = take_v_s()
+            picks = list1[:, c * CH // 16 : (c + 1) * CH // 16]
+            nc.vector.tensor_copy(out=v_w[c][:], in_=tab_w[:].bitcast(U32).indirect(picks))
+            nc.vector.tensor_copy(out=v_s[c][:], in_=tab_s[:].indirect(picks))
+
+        w2_w = kept("w2_w", [P, 2 * M], U8)
+        w2_s = kept("w2_s", [P, M], U8)
+        for quad in range(4):
+            live = slice(32 * quad, 32 * quad + 4)
+            nc.vector.tensor_copy(out=w2_s_plane[live, :].bitcast(I32), in_=w2_s_raw[live, :].bitcast(I32))
+        for b in range(2):
+            nc.vector.tensor_copy(
+                out=w2_s[:, 512 * b : 512 * (b + 1)].rearrange("p (t q) -> p q t", t=4),
+                in_=w2_s_plane[:, 512 * b : 512 * (b + 1)].rearrange("p (q t) -> p q t", t=4),
+            )
+            nc.vector.tensor_copy(
+                out=w2_w[:, 1024 * b : 1024 * (b + 1)].rearrange("p (t q e) -> p q t e", t=4, e=2),
+                in_=w2_raw[:].bitcast(U8)[:, 1024 * b : 1024 * (b + 1)].rearrange("p (q t e) -> p q t e", t=4, e=2),
+            )
+
+        def quantise(src_bf, codes, scales):
+            nc.vector.quantize_mx(out=codes.bitcast(FP8X4), scales=scales, in_=src_bf)
+
+        take_w_bf = ring("w_bf", 2, [P, 2048], BF16)
+
+        def prepare_weight(name, raw, copy):
+            grouped = take_w_bf()
+            copy(
+                out=grouped[:].rearrange("p (t q j) -> p q t j", t=4, j=4),
+                in_=raw[:].rearrange("p j (q t) -> p q t j", t=4),
+            )
+            codes = kept(name + "_w", [P, 512], U32)
+            scales = kept(name + "_s", [P, 512], U8)
+            quantise(grouped[:], codes[:], scales[:])
+            return codes, scales
+
+        w1_q = {}
+        w3_q = {}
+        ratio_w = {}
+        ratio_s = {}
+        take_irr = bank_ring(IRR_BANKS)
+        take_curv = bank_ring(CURV_BANKS)
+        take_damp = ring("damp", DAMP_RING, [P, UW * 4], F32)
+        take_ratio_bf = ring("ratio_bf", 2, [P, CH * 4], BF16)
+
+        def ratio_pass(c, b):
+            damp = []
+            for u in range(CH // UW):
+                cols = slice(u * UW, (u + 1) * UW)
+                irr = take_irr()
+                for t in range(4):
+                    col = 512 * b + 128 * t
+                    nc.tensor.matmul_mx(
+                        out=irr[:, UW * t : UW * (t + 1)],
+                        lhsT=w2_w[:, 2 * col : 2 * (col + 128)].bitcast(FP4X4),
+                        lhsT_scale=w2_s[:, col : col + 128],
+                        rhs=v_w[c][:, cols].bitcast(FP8X4),
+                        rhs_scale=v_s[c][:, cols],
+                        start=True,
+                        stop=True,
+                    )
+                d = take_damp()
+                nc.scalar.activation(
+                    out=d[:].rearrange("p (j t) -> p j t", t=4),
+                    in_=irr[:].rearrange("p (t j) -> p j t", t=4),
+                    func=ACT.Abs,
+                )
+                damp.append(d)
+            for d in damp:
+                nc.scalar.activation(out=d[:], in_=d[:], func=ACT.Abs_reciprocal_sqrt, bias=1.0)
+            for d in damp:
+                nc.scalar.activation(out=d[:], in_=d[:], func=ACT.Square)
+            if (c, b) == (NCH - 1, 1) and SIN_WARM:
+                nc.scalar.activation(out=warm[:, 2:3], in_=damp[-1][:, 0:1], func=ACT.Sin)
+            ratio_bf = take_ratio_bf()
+            for u in range(CH // UW):
+                cols = slice(u * UW, (u + 1) * UW)
+                curv = take_curv()
+                for t in range(4):
+                    nc.tensor.matmul_mx(
+                        out=curv[:, UW * t : UW * (t + 1)],
+                        lhsT=w1_q[b][0][:, 128 * t : 128 * (t + 1)].bitcast(FP8X4),
+                        lhsT_scale=w1_q[b][1][:, 128 * t : 128 * (t + 1)],
+                        rhs=v_w[c][:, cols].bitcast(FP8X4),
+                        rhs_scale=v_s[c][:, cols],
+                        start=True,
+                        stop=True,
+                    )
+                nc.vector.tensor_tensor(
+                    out=ratio_bf[:, u * UW * 4 : (u + 1) * UW * 4].rearrange("p (j t) -> p j t", t=4),
+                    in0=curv[:].rearrange("p (t j) -> p j t", t=4),
+                    in1=damp[u][:].rearrange("p (j t) -> p j t", t=4),
+                    op=ALU.mult,
+                )
+            ratio_w[c, b] = kept(f"ratio_w{c}_{b}", [P, CH], U32)
+            ratio_s[c, b] = kept(f"ratio_s{c}_{b}", [P, CH], U8)
+            quantise(ratio_bf[:], ratio_w[c, b][:], ratio_s[c, b][:])
+
+        def h_rows(c, tiles, acc, dst):
+            for i, t in enumerate(tiles):
+                for b in range(2):
+                    nc.tensor.matmul_mx(
+                        out=acc[:, CH * i : CH * (i + 1)],
+                        lhsT=w3_q[b][0][:, 128 * t : 128 * (t + 1)].bitcast(FP8X4),
+                        lhsT_scale=w3_q[b][1][:, 128 * t : 128 * (t + 1)],
+                        rhs=ratio_w[c, b][:].bitcast(FP8X4),
+                        rhs_scale=ratio_s[c, b][:],
+                        start=(b == 0),
+                        stop=(b == 1),
+                    )
+            width = CH * len(tiles)
+            nc.scalar.copy(out=dst[:, 0:width], in_=acc[:, 0:width])
+
+        def put(c, t, h_ap):
+            places = list2[:, c * CH // 16 : (c + 1) * CH // 16]
+            nc.vector.tensor_tensor(
+                out=page[t][:].indirect(places), in0=h_ap, in1=wgs_sb[t, c // 2][:, c % 2 * CH : (c % 2 + 1) * CH], op=ALU.mult
+            )
+
+        take_early_bank = bank_ring(EARLY_BANKS)
+        take_late_bank = bank_ring(LATE_BANKS)
+        take_early = ring("h_early", EARLY_RING, [P, 2 * CH], F32)
+        take_handed = ring("handed", HAND_RING, [P, CH], F32)
+
+        def early_h(c):
+            dst = take_early()
+            h_rows(c, [0, 1], take_early_bank(), dst)
+            return dst
+
+        late = {}
+
+        def late_h(c, t, dst=None):
+            late[c, t] = take_handed() if dst is None else dst
+            h_rows(c, [t], take_late_bank(), late[c, t])
+
+        def late_put(c, t):
+            put(c, t, late[c, t][:, 0:CH])
+
+        vcopy, scopy = nc.vector.tensor_copy, nc.scalar.copy
+        gather_table(0)
+        w1_q[0] = prepare_weight("w1_0", w1_raw[0], CASTS[0] == "v" and vcopy or scopy)
+        ratio_pass(0, 0)
+        w1_q[1] = prepare_weight("w1_1", w1_raw[1], CASTS[1] == "v" and vcopy or scopy)
+        gather_table(1)
+        ratio_pass(0, 1)
+        w3_q[0] = prepare_weight("w3_0", w3_raw[0], CASTS[2] == "v" and vcopy or scopy)
+        w3_q[1] = prepare_weight("w3_1", w3_raw[1], CASTS[3] == "v" and vcopy or scopy)
+        for c in range(NCH - 1):
+            if c + 2 < NCH:
+                gather_table(c + 2)
+            ratio_pass(c + 1, 0)
+            ratio_pass(c + 1, 1)
+            h01 = early_h(c)
+            put(c, 0, h01[:, 0:CH])
+            put(c, 1, h01[:, CH : 2 * CH])
+
+        w4_w = kept("w4_w", [P, H], I32)
+        w4_s = kept("w4_s", [P, H], U8)
+
+        def deal_w4():
+            nc.vector.tensor_copy(
+                out=w4_w[:].rearrange("p (t q) -> p q t", t=4), in_=w4_raw[:].rearrange("p (q t) -> p q t", t=4)
+            )
+            nc.vector.tensor_copy(
+                out=w4_s[:].rearrange("p (t q) -> p q t", t=4), in_=w4_s_raw[:].rearrange("p (q t) -> p q t", t=4)
+            )
+
+        out_rows = out.rearrange("(p t) j -> p t j", t=4)
+        x_bf = [kept(f"x_bf{q}", [P, QW * 4], BF16) for q in range(PN // QW)]
+        take_turns = ring("turns", TURN_RING, [P, HW], F32)
+        take_rest = ring("rest", REST_RING, [P, HW], F32)
+        turns = {}
+
+        def pick(t, h):
+            picks = list3[:, h * HW // 16 : (h + 1) * HW // 16]
+            turns[t, h] = take_turns()
+            nc.vector.tensor_scalar(
+                out=turns[t, h][:], in0=page[t][:].indirect(picks), scalar1=1.0 / (2.0 * math.pi), scalar2=0.0,
+                op0=ALU.mult, op1=ALU.add,
+            )
+
+        whole = {}
+        rest = {}
+        take_whole = ring("whole", WHOLE_RING, [P, HW], U32)
+
+        def round_turns(t, h, cols=slice(0, HW)):
+            if cols.start == 0:
+                whole[t, h] = take_whole()
+            nc.scalar.activation(out=whole[t, h][:, cols], in_=turns[t, h][:, cols], func=ACT.Copy, bias=ROUNDER)
+
+        def reduce(t, h, cols=slice(0, HW)):
+            if cols.start == 0:
+                rest[t, h] = take_rest()
+            nc.vector.scalar_tensor_tensor(
+                out=rest[t, h][:, cols], in0=whole[t, h][:, cols].bitcast(I32), scalar=ROUNDER, in1=turns[t, h][:, cols],
+                op0=ALU.subtract, op1=ALU.subtract,
+            )
+
+        def sine(t, h, cols=slice(0, HW)):
+            nc.scalar.activation(out=rest[t, h][:, cols], in_=rest[t, h][:, cols], func=ACT.Sin, scale=-2.0 * math.pi)
+
+        x_rows = [kept(f"x_rows{h}", [P, 3, HW], BF16) for h in range(PN // HW)]
+
+        def scale_row(t, h):
+            nc.scalar.activation(out=x_rows[h][:, t, :], in_=rest[t, h][:], func=ACT.Copy, scale=gain_sb[:, t : t + 1])
+
+        def weave(q):
+            h, i = divmod(q, HW // QW)
+            nc.scalar.copy(
+                out=x_bf[q][:].rearrange("p (j t) -> p j t", t=4)[:, :, 0:3],
+                in_=x_rows[h][:, :, i * QW : (i + 1) * QW].rearrange("p t j -> p j t"),
+            )
+
+        def scale(t, h, cols=slice(0, HW)):
+            for i in range(cols.start // QW, cols.stop // QW):
+                dst = x_bf[h * (HW // QW) + i][:].rearrange("p (j t) -> p t j", t=4)[:, t, :]
+                src = rest[t, h][:, i * QW : (i + 1) * QW]
+                if (t, h) in GAIN_ON_VECTOR:
+                    nc.vector.tensor_scalar(out=dst, in0=src, scalar1=gain_sb[:, t : t + 1], scalar2=None, op0=ALU.mult)
+                else:
+                    nc.scalar.activation(out=dst, in_=src, func=ACT.Copy, scale=gain_sb[:, t : t + 1])
+
+        take_y_bank = bank_ring(Y_BANKS)
+        take_x_w = ring("x_w", 2, [P, QW], U32)
+        take_x_s = ring("x_s", 2, [P, QW], U8)
+        take_y = ring("y_sb", Y_RING, [P, QW], F32)
+        take_result = ring("result", RES_RING, [P, 2, QW], F32)
+        accs = {}
+
+        def last_product(q):
+            x_w = take_x_w()
+            x_s = take_x_s()
+            quantise(x_bf[q][:], x_w[:], x_s[:])
+            for pair in range(2):
+                acc = take_y_bank()
+                accs[q, pair] = acc
+                for i in range(2):
+                    t = 2 * pair + i
+                    nc.tensor.matmul_mx(
+                        out=acc[:, QW * i : QW * (i + 1)],
+                        lhsT=w4_w[:, 128 * t : 128 * (t + 1)].bitcast(FP8X4),
+                        lhsT_scale=w4_s[:, 128 * t : 128 * (t + 1)],
+                        rhs=x_w[:].bitcast(FP8X4),
+                        rhs_scale=x_s[:],
+                        start=True,
+                        stop=True,
+                    )
+
+        def finish(q):
+            picks = list4[:, q * QW // 16 : (q + 1) * QW // 16]
+            for pair in range(2):
+                result = take_result()
+                for i in range(2):
+                    t = 2 * pair + i
+                    y_sb = take_y()
+                    nc.scalar.activation(
+                        out=y_sb[:], in_=accs[q, pair][:, QW * i : QW * (i + 1)], func=ACT.Identity, bias=base_sb[:, t : t + 1]
+                    )
+                    nc.vector.tensor_tensor(out=result[:, i, :], in0=page[t][:].indirect(picks), in1=y_sb[:], op=ALU.mult)
+                nc.sync.dma_start(out=out_rows[:, 2 * pair : 2 * pair + 2, q * QW : (q + 1) * QW], in_=result[:])
+
+        last = NCH - 1
+        late_h(0, 2)
+        late_h(1, 2)
+        late_put(0, 2)
+        late_put(1, 2)
+        h01 = early_h(last)
+        put(last, 0, h01[:, 0:CH])
+        put(last, 1, h01[:, CH : 2 * CH])
+        held = h01[:, 0:CH]
+        late_h(2, 2, held)
+        for t in range(3):
+            pick(t, 0)
+            pick(t, 1)
+            late_put(*[(2, 2), (3, 2), (0, 3)][t])
+            round_turns(t, 0)
+            round_turns(t, 1)
+            late_h(*[(3, 2), (0, 3), (1, 3)][t], held)
+            if t > 0:
+                sine(t - 1, 1)
+                scale_row(t - 1, 1)
+            reduce(t, 0)
+            reduce(t, 1)
+            if t == 2:
+                late_h(2, 3, turns[2, 1][:])
+            sine(t, 0)
+            scale_row(t, 0)
+        late_put(1, 3)
+        late_h(3, 3, held)
+        weave(0)
+        weave(1)
+        sine(2, 1)
+        scale_row(2, 1)
+        weave(2)
+        weave(3)
+        late_put(2, 3)
+        late_put(3, 3)
+        deal_w4()
+        pick(3, 0)
+        pick(3, 1)
+        first, second = slice(0, QW), slice(QW, HW)
+        round_turns(3, 0, first)
+        round_turns(3, 0, second)
+        reduce(3, 0, first)
+        reduce(3, 0, second)
+        round_turns(3, 1)
+        sine(3, 0, first)
+        scale(3, 0, first)
+        reduce(3, 1)
+        last_product(0)
+        sine(3, 0, second)
+        scale(3, 0, second)
+        last_product(1)
+        finish(0)
+        sine(3, 1)
+        scale(3, 1)
+        finish(1)
+        last_product(2)
+        last_product(3)
+        finish(2)
+        finish(3)

@@ -2,6 +2,7 @@ import math
 from contextlib import ExitStack
 
 import concourse.mybir as mybir
+from concourse.masks import make_identity
 
 K, M, H, T, S, T2, PN = 512, 1024, 512, 2048, 1024, 2048, 1024
 FLOPS = 2 * (2 * K * M * S + M * H * S + H * H * PN)
@@ -27,7 +28,7 @@ ROUNDER = 12582912.0
 SMALL_AFTER = 1
 V_RING = 3
 IRR_BANKS = [0,1,2]
-CURV_BANKS = [3,4,6,7]
+CURV_BANKS = [3,4,7]
 EARLY_BANKS = [5]
 LATE_BANKS = [6,7]
 Y_BANKS = [0,1,2,3]
@@ -35,13 +36,17 @@ DAMP_RING = 6
 EARLY_RING = 4
 HAND_RING = 2
 TURN_RING = 2
-REST_RING = 3
+REST_RING = 2
 Y_RING = 4
 RES_RING = 4
 CASTS = "vvvv"
 GAIN_ON_VECTOR = ((3, 0), (3, 1))
 WHOLE_RING = 2
 SIN_WARM = 1
+H_BANKS = [5,6]
+T_BANKS = [0,1]
+B_BANKS = [2,3]
+M_RING = 2
 
 
 def tile_list_fellow_eye_fitting_kernel(
@@ -101,7 +106,7 @@ def tile_list_fellow_eye_fitting_kernel(
 
         list1 = load_list("list1", offs)
         w2_s_raw = kept("w2_s_raw", [P, M], U8)
-        load_plane(w2_s_raw, w2_scales, nc.scalar)
+        load_plane(w2_s_raw, w2_scales, nc.sync)
         w2_raw = kept("w2_raw", [P, M // 2], I32)
         nc.sync.dma_start(out=w2_raw[:], in_=w2_words[0].bitcast(I32))
         tab_w = kept("tab_w", [P, T], I32)
@@ -122,8 +127,8 @@ def tile_list_fellow_eye_fitting_kernel(
         page_rows = page0.rearrange("(p t) c -> p t c", t=4)
         page = [kept(f"page{t}", [P, T2], F32) for t in range(4)]
 
-        def load_wgs(t, half):
-            wgs_sb[t, half] = kept(f"wgs{t}_{half}", [P, S // 2], F32)
+        def load_wgs(t, half, into=None):
+            wgs_sb[t, half] = kept(f"wgs{t}_{half}", [P, S // 2], F32) if into is None else into
             for quad in range(4):
                 nc.sync.dma_start(
                     out=wgs_sb[t, half][32 * quad : 32 * (quad + 1)],
@@ -144,17 +149,15 @@ def tile_list_fellow_eye_fitting_kernel(
             load_plane(w4_s_raw, w4_scales, nc.sync)
             return raw
 
-        for t in range(3):
+        for t in range(2):
             load_wgs(t, 0)
             load_page(t)
-        load_wgs(0, 1)
-        load_wgs(1, 1)
+        for t in range(2):
+            load_wgs(t, 1)
         list3 = load_list("list3", offs3)
         gain_sb = load_column("gain_sb", gain)
-        load_wgs(2, 1)
-        load_wgs(3, 0)
+        load_page(2)
         load_page(3)
-        load_wgs(3, 1)
         list4 = load_list("list4", offs4)
         base_sb = load_column("base_sb", base)
         w4_raw = load_w4()
@@ -182,8 +185,8 @@ def tile_list_fellow_eye_fitting_kernel(
                 in_=w2_s_plane[:, 512 * b : 512 * (b + 1)].rearrange("p (q t) -> p q t", t=4),
             )
             nc.vector.tensor_copy(
-                out=w2_w[:, 1024 * b : 1024 * (b + 1)].rearrange("p (t q e) -> p q t e", t=4, e=2),
-                in_=w2_raw[:].bitcast(U8)[:, 1024 * b : 1024 * (b + 1)].rearrange("p (q t e) -> p q t e", t=4, e=2),
+                out=w2_w[:].bitcast(U16)[:, 512 * b : 512 * (b + 1)].rearrange("p (t q) -> p q t", t=4),
+                in_=w2_raw[:].bitcast(U16)[:, 512 * b : 512 * (b + 1)].rearrange("p (q t) -> p q t", t=4),
             )
 
         def quantise(src_bf, codes, scales):
@@ -276,33 +279,23 @@ def tile_list_fellow_eye_fitting_kernel(
                         start=(b == 0),
                         stop=(b == 1),
                     )
-            width = CH * len(tiles)
-            nc.scalar.copy(out=dst[:, 0:width], in_=acc[:, 0:width])
+            nc.scalar.copy(out=dst, in_=acc[:].rearrange("p (i j) -> p i j", i=2))
 
-        def put(c, t, h_ap):
-            places = list2[:, c * CH // 16 : (c + 1) * CH // 16]
+        take_h_bank = bank_ring(H_BANKS)
+        h_sb = [kept(f"h{pair}", [P, 2, S], F32) for pair in range(2)]
+
+        def make_h(c, pair):
+            h_rows(c, [2 * pair, 2 * pair + 1], take_h_bank(), h_sb[pair][:, :, c * CH : (c + 1) * CH])
+
+        def put_rows(c, t, count=1):
+            first, width = c * CH, count * CH
+            half, at = divmod(first, S // 2)
             nc.vector.tensor_tensor(
-                out=page[t][:].indirect(places), in0=h_ap, in1=wgs_sb[t, c // 2][:, c % 2 * CH : (c % 2 + 1) * CH], op=ALU.mult
+                out=page[t][:].indirect(list2[:, first // 16 : (first + width) // 16]),
+                in0=h_sb[t // 2][:, t % 2, first : first + width],
+                in1=wgs_sb[t, half][:, at : at + width],
+                op=ALU.mult,
             )
-
-        take_early_bank = bank_ring(EARLY_BANKS)
-        take_late_bank = bank_ring(LATE_BANKS)
-        take_early = ring("h_early", EARLY_RING, [P, 2 * CH], F32)
-        take_handed = ring("handed", HAND_RING, [P, CH], F32)
-
-        def early_h(c):
-            dst = take_early()
-            h_rows(c, [0, 1], take_early_bank(), dst)
-            return dst
-
-        late = {}
-
-        def late_h(c, t, dst=None):
-            late[c, t] = take_handed() if dst is None else dst
-            h_rows(c, [t], take_late_bank(), late[c, t])
-
-        def late_put(c, t):
-            put(c, t, late[c, t][:, 0:CH])
 
         vcopy, scopy = nc.vector.tensor_copy, nc.scalar.copy
         gather_table(0)
@@ -318,9 +311,9 @@ def tile_list_fellow_eye_fitting_kernel(
                 gather_table(c + 2)
             ratio_pass(c + 1, 0)
             ratio_pass(c + 1, 1)
-            h01 = early_h(c)
-            put(c, 0, h01[:, 0:CH])
-            put(c, 1, h01[:, CH : 2 * CH])
+            make_h(c, 0)
+            for t in range(2):
+                put_rows(c, t)
 
         w4_w = kept("w4_w", [P, H], I32)
         w4_s = kept("w4_s", [P, H], U8)
@@ -335,58 +328,84 @@ def tile_list_fellow_eye_fitting_kernel(
 
         out_rows = out.rearrange("(p t) j -> p t j", t=4)
         x_bf = [kept(f"x_bf{q}", [P, QW * 4], BF16) for q in range(PN // QW)]
-        take_turns = ring("turns", TURN_RING, [P, HW], F32)
-        take_rest = ring("rest", REST_RING, [P, HW], F32)
+        take_turns = ring("turns", TURN_RING, [P, PN], F32)
+        take_whole = ring("whole", WHOLE_RING, [P, PN], U32)
+        take_rest = ring("rest", REST_RING, [P, PN], F32)
+        x_rows = kept("x_rows", [P, 3, PN], BF16)
         turns = {}
-
-        def pick(t, h):
-            picks = list3[:, h * HW // 16 : (h + 1) * HW // 16]
-            turns[t, h] = take_turns()
-            nc.vector.tensor_scalar(
-                out=turns[t, h][:], in0=page[t][:].indirect(picks), scalar1=1.0 / (2.0 * math.pi), scalar2=0.0,
-                op0=ALU.mult, op1=ALU.add,
-            )
-
         whole = {}
         rest = {}
-        take_whole = ring("whole", WHOLE_RING, [P, HW], U32)
 
-        def round_turns(t, h, cols=slice(0, HW)):
-            if cols.start == 0:
-                whole[t, h] = take_whole()
-            nc.scalar.activation(out=whole[t, h][:, cols], in_=turns[t, h][:, cols], func=ACT.Copy, bias=ROUNDER)
+        def pick(t):
+            turns[t] = take_turns()
+            whole[t] = take_whole()
+            rest[t] = take_rest()
+            for a in range(0, PN, HW):
+                nc.vector.tensor_scalar(
+                    out=turns[t][:, a : a + HW], in0=page[t][:].indirect(list3[:, a // 16 : (a + HW) // 16]),
+                    scalar1=1.0 / (2.0 * math.pi), scalar2=0.0, op0=ALU.mult, op1=ALU.add,
+                )
 
-        def reduce(t, h, cols=slice(0, HW)):
-            if cols.start == 0:
-                rest[t, h] = take_rest()
+        def round_turns(t, cols):
+            nc.scalar.activation(out=whole[t][:, cols], in_=turns[t][:, cols], func=ACT.Copy, bias=ROUNDER)
+
+        def reduce(t, cols):
             nc.vector.scalar_tensor_tensor(
-                out=rest[t, h][:, cols], in0=whole[t, h][:, cols].bitcast(I32), scalar=ROUNDER, in1=turns[t, h][:, cols],
+                out=rest[t][:, cols], in0=whole[t][:, cols].bitcast(I32), scalar=ROUNDER, in1=turns[t][:, cols],
                 op0=ALU.subtract, op1=ALU.subtract,
             )
 
-        def sine(t, h, cols=slice(0, HW)):
-            nc.scalar.activation(out=rest[t, h][:, cols], in_=rest[t, h][:, cols], func=ACT.Sin, scale=-2.0 * math.pi)
+        def sine(t, cols):
+            nc.scalar.activation(out=rest[t][:, cols], in_=rest[t][:, cols], func=ACT.Sin, scale=-2.0 * math.pi)
 
-        x_rows = [kept(f"x_rows{h}", [P, 3, HW], BF16) for h in range(PN // HW)]
+        identity = kept("identity", [P, P], F32)
+        make_identity(nc, identity[:])
+        take_turn_bank = bank_ring(T_BANKS)
+        take_back_bank = bank_ring(B_BANKS)
+        take_minus = ring("minus_whole", M_RING, [P, HW], F32)
+        take_sine = ring("sine_t", M_RING, [P, HW], F32)
+        minus = {}
+        sine_t = {}
 
-        def scale_row(t, h):
-            nc.scalar.activation(out=x_rows[h][:, t, :], in_=rest[t, h][:], func=ACT.Copy, scale=gain_sb[:, t : t + 1])
+        def negate(t, cols):
+            minus[t, cols.start] = take_minus()
+            nc.scalar.activation(out=minus[t, cols.start][:], in_=whole[t][:, cols], func=ACT.Copy, scale=-1.0, bias=ROUNDER)
+
+        def sine_turned(t, cols):
+            bank = take_turn_bank()
+            for a in range(0, HW, P):
+                nc.tensor.matmul(
+                    out=bank[:, a : a + P], lhsT=turns[t][:, cols.start + a : cols.start + a + P], rhs=identity[:],
+                    start=(a == 0), stop=False, is_transpose=True,
+                )
+            for a in range(0, HW, P):
+                nc.tensor.matmul(
+                    out=bank[:, a : a + P], lhsT=minus[t, cols.start][:, a : a + P], rhs=identity[:],
+                    start=False, stop=(a == HW - P), is_transpose=True,
+                )
+            sine_t[t, cols.start] = take_sine()
+            nc.scalar.activation(out=sine_t[t, cols.start][:], in_=bank[:], func=ACT.Sin, scale=2.0 * math.pi)
+
+        def scale_back(t, cols):
+            bank = take_back_bank()
+            for a in range(0, HW, P):
+                nc.tensor.transpose(bank[:, a : a + P], sine_t[t, cols.start][:, a : a + P], identity[:])
+            nc.scalar.activation(out=x_rows[:, t, cols], in_=bank[:], func=ACT.Copy, scale=gain_sb[:, t : t + 1])
+
+        def scale_row(t, cols):
+            nc.scalar.activation(out=x_rows[:, t, cols], in_=rest[t][:, cols], func=ACT.Copy, scale=gain_sb[:, t : t + 1])
 
         def weave(q):
-            h, i = divmod(q, HW // QW)
             nc.scalar.copy(
                 out=x_bf[q][:].rearrange("p (j t) -> p j t", t=4)[:, :, 0:3],
-                in_=x_rows[h][:, :, i * QW : (i + 1) * QW].rearrange("p t j -> p j t"),
+                in_=x_rows[:, :, q * QW : (q + 1) * QW].rearrange("p t j -> p j t"),
             )
 
-        def scale(t, h, cols=slice(0, HW)):
-            for i in range(cols.start // QW, cols.stop // QW):
-                dst = x_bf[h * (HW // QW) + i][:].rearrange("p (j t) -> p t j", t=4)[:, t, :]
-                src = rest[t, h][:, i * QW : (i + 1) * QW]
-                if (t, h) in GAIN_ON_VECTOR:
-                    nc.vector.tensor_scalar(out=dst, in0=src, scalar1=gain_sb[:, t : t + 1], scalar2=None, op0=ALU.mult)
-                else:
-                    nc.scalar.activation(out=dst, in_=src, func=ACT.Copy, scale=gain_sb[:, t : t + 1])
+        def scale_last(q):
+            nc.vector.tensor_scalar(
+                out=x_bf[q][:].rearrange("p (j t) -> p t j", t=4)[:, 3, :], in0=rest[3][:, q * QW : (q + 1) * QW],
+                scalar1=gain_sb[:, 3:4], scalar2=None, op0=ALU.mult,
+            )
 
         take_y_bank = bank_ring(Y_BANKS)
         take_x_w = ring("x_w", 2, [P, QW], U32)
@@ -428,60 +447,59 @@ def tile_list_fellow_eye_fitting_kernel(
                 nc.sync.dma_start(out=out_rows[:, 2 * pair : 2 * pair + 2, q * QW : (q + 1) * QW], in_=result[:])
 
         last = NCH - 1
-        late_h(0, 2)
-        late_h(1, 2)
-        late_put(0, 2)
-        late_put(1, 2)
-        h01 = early_h(last)
-        put(last, 0, h01[:, 0:CH])
-        put(last, 1, h01[:, CH : 2 * CH])
-        held = h01[:, 0:CH]
-        late_h(2, 2, held)
-        for t in range(3):
-            pick(t, 0)
-            pick(t, 1)
-            late_put(*[(2, 2), (3, 2), (0, 3)][t])
-            round_turns(t, 0)
-            round_turns(t, 1)
-            late_h(*[(3, 2), (0, 3), (1, 3)][t], held)
-            if t > 0:
-                sine(t - 1, 1)
-                scale_row(t - 1, 1)
-            reduce(t, 0)
-            reduce(t, 1)
-            if t == 2:
-                late_h(2, 3, turns[2, 1][:])
-            sine(t, 0)
-            scale_row(t, 0)
-        late_put(1, 3)
-        late_h(3, 3, held)
-        weave(0)
-        weave(1)
-        sine(2, 1)
-        scale_row(2, 1)
-        weave(2)
-        weave(3)
-        late_put(2, 3)
-        late_put(3, 3)
+        halves = [slice(0, HW), slice(HW, PN)]
+        quarters = [slice(q * QW, (q + 1) * QW) for q in range(4)]
+        make_h(last, 0)
+        for c in range(NCH):
+            make_h(c, 1)
+        for t in range(4):
+            if t < 2:
+                put_rows(last, t)
+                load_wgs(2, t, wgs_sb[t, 1])
+            elif t == 2:
+                for half in range(2):
+                    put_rows(2 * half, 2, 2)
+                    load_wgs(3, half, wgs_sb[2, half])
+            if t < 3:
+                pick(t)
+                for cols in halves:
+                    round_turns(t, cols)
+                    if t in (0, 1):
+                        negate(t, cols)
+            if t - 1 in (0, 1):
+                scale_back(t - 1, halves[1])
+            elif t > 0:
+                reduce(t - 1, slice(0, PN))
+                for cols in halves:
+                    sine(t - 1, cols)
+                for cols in halves:
+                    scale_row(t - 1, cols)
+            if t in (0, 1):
+                for cols in halves:
+                    sine_turned(t, cols)
+                scale_back(t, halves[0])
+        for q in range(4):
+            weave(q)
+        put_rows(0, 3, 2)
+        put_rows(2, 3, 2)
         deal_w4()
-        pick(3, 0)
-        pick(3, 1)
-        first, second = slice(0, QW), slice(QW, HW)
-        round_turns(3, 0, first)
-        round_turns(3, 0, second)
-        reduce(3, 0, first)
-        reduce(3, 0, second)
-        round_turns(3, 1)
-        sine(3, 0, first)
-        scale(3, 0, first)
-        reduce(3, 1)
+        pick(3)
+        round_turns(3, quarters[0])
+        round_turns(3, quarters[1])
+        reduce(3, quarters[0])
+        reduce(3, quarters[1])
+        round_turns(3, halves[1])
+        sine(3, quarters[0])
+        scale_last(0)
+        reduce(3, halves[1])
         last_product(0)
-        sine(3, 0, second)
-        scale(3, 0, second)
+        sine(3, quarters[1])
+        scale_last(1)
         last_product(1)
         finish(0)
-        sine(3, 1)
-        scale(3, 1)
+        sine(3, halves[1])
+        scale_last(2)
+        scale_last(3)
         finish(1)
         last_product(2)
         last_product(3)

@@ -31,7 +31,7 @@ IRR_BANKS = [0,1,2]
 CURV_BANKS = [3,4,7]
 EARLY_BANKS = [5]
 LATE_BANKS = [6,7]
-Y_BANKS = [0,1,2,3]
+Y_BANKS = [0,1,2,3,4,5,6,7]
 DAMP_RING = 6
 EARLY_RING = 4
 HAND_RING = 2
@@ -44,9 +44,10 @@ GAIN_ON_VECTOR = ((3, 0), (3, 1))
 WHOLE_RING = 2
 SIN_WARM = 1
 H_BANKS = [5,6]
-T_BANKS = [0,1]
-B_BANKS = [2,3]
+T_BANKS = [3,4]
+B_BANKS = [7,0]
 M_RING = 2
+PIECES = [[0,256],[256,512],[512,1024]]
 
 
 def tile_list_fellow_eye_fitting_kernel(
@@ -127,13 +128,12 @@ def tile_list_fellow_eye_fitting_kernel(
         page_rows = page0.rearrange("(p t) c -> p t c", t=4)
         page = [kept(f"page{t}", [P, T2], F32) for t in range(4)]
 
-        def load_wgs(t, half, into=None):
-            wgs_sb[t, half] = kept(f"wgs{t}_{half}", [P, S // 2], F32) if into is None else into
+        def load_wgs(t, first, width, into):
+            wgs_sb[t, first] = into
             for quad in range(4):
-                nc.sync.dma_start(
-                    out=wgs_sb[t, half][32 * quad : 32 * (quad + 1)],
-                    in_=wgs_rows[:, t, half * S // 2 : (half + 1) * S // 2],
-                )
+                nc.sync.dma_start(out=into[32 * quad : 32 * (quad + 1), 0:width], in_=wgs_rows[:, t, first : first + width])
+
+        wgs_tiles = [kept(f"wgs{i}", [P, 3 * CH if i == 3 else 2 * CH], F32) for i in range(4)]
 
         def load_page(t):
             nc.sync.dma_start(out=page[t][:], in_=page_rows[:, t, :])
@@ -150,17 +150,17 @@ def tile_list_fellow_eye_fitting_kernel(
             return raw
 
         for t in range(2):
-            load_wgs(t, 0)
+            load_wgs(t, 0, 2 * CH, wgs_tiles[t])
             load_page(t)
         for t in range(2):
-            load_wgs(t, 1)
+            load_wgs(t, 2 * CH, 2 * CH, wgs_tiles[2 + t])
+        w4_raw = load_w4()
         list3 = load_list("list3", offs3)
         gain_sb = load_column("gain_sb", gain)
         load_page(2)
         load_page(3)
         list4 = load_list("list4", offs4)
         base_sb = load_column("base_sb", base)
-        w4_raw = load_w4()
 
         v_w = {}
         v_s = {}
@@ -212,7 +212,8 @@ def tile_list_fellow_eye_fitting_kernel(
         take_irr = bank_ring(IRR_BANKS)
         take_curv = bank_ring(CURV_BANKS)
         take_damp = ring("damp", DAMP_RING, [P, UW * 4], F32)
-        take_ratio_bf = ring("ratio_bf", 2, [P, CH * 4], BF16)
+        take_ratio_bf = ring("ratio_bf", 2, [P, 2 * CH * 4], BF16)
+        ratio_bf = {}
 
         def ratio_pass(c, b):
             damp = []
@@ -243,7 +244,8 @@ def tile_list_fellow_eye_fitting_kernel(
                 nc.scalar.activation(out=d[:], in_=d[:], func=ACT.Square)
             if (c, b) == (NCH - 1, 1) and SIN_WARM:
                 nc.scalar.activation(out=warm[:, 2:3], in_=damp[-1][:, 0:1], func=ACT.Sin)
-            ratio_bf = take_ratio_bf()
+            if b == 0:
+                ratio_bf[c] = take_ratio_bf()
             for u in range(CH // UW):
                 cols = slice(u * UW, (u + 1) * UW)
                 curv = take_curv()
@@ -258,14 +260,15 @@ def tile_list_fellow_eye_fitting_kernel(
                         stop=True,
                     )
                 nc.vector.tensor_tensor(
-                    out=ratio_bf[:, u * UW * 4 : (u + 1) * UW * 4].rearrange("p (j t) -> p j t", t=4),
+                    out=ratio_bf[c][:, (b * CH + u * UW) * 4 : (b * CH + (u + 1) * UW) * 4].rearrange("p (j t) -> p j t", t=4),
                     in0=curv[:].rearrange("p (t j) -> p j t", t=4),
                     in1=damp[u][:].rearrange("p (j t) -> p j t", t=4),
                     op=ALU.mult,
                 )
-            ratio_w[c, b] = kept(f"ratio_w{c}_{b}", [P, CH], U32)
-            ratio_s[c, b] = kept(f"ratio_s{c}_{b}", [P, CH], U8)
-            quantise(ratio_bf[:], ratio_w[c, b][:], ratio_s[c, b][:])
+            if b == 1:
+                ratio_w[c] = kept(f"ratio_w{c}", [P, 2 * CH], U32)
+                ratio_s[c] = kept(f"ratio_s{c}", [P, 2 * CH], U8)
+                quantise(ratio_bf[c][:], ratio_w[c][:], ratio_s[c][:])
 
         def h_rows(c, tiles, acc, dst):
             for i, t in enumerate(tiles):
@@ -274,8 +277,8 @@ def tile_list_fellow_eye_fitting_kernel(
                         out=acc[:, CH * i : CH * (i + 1)],
                         lhsT=w3_q[b][0][:, 128 * t : 128 * (t + 1)].bitcast(FP8X4),
                         lhsT_scale=w3_q[b][1][:, 128 * t : 128 * (t + 1)],
-                        rhs=ratio_w[c, b][:].bitcast(FP8X4),
-                        rhs_scale=ratio_s[c, b][:],
+                        rhs=ratio_w[c][:, b * CH : (b + 1) * CH].bitcast(FP8X4),
+                        rhs_scale=ratio_s[c][:, b * CH : (b + 1) * CH],
                         start=(b == 0),
                         stop=(b == 1),
                     )
@@ -284,16 +287,17 @@ def tile_list_fellow_eye_fitting_kernel(
         take_h_bank = bank_ring(H_BANKS)
         h_sb = [kept(f"h{pair}", [P, 2, S], F32) for pair in range(2)]
 
-        def make_h(c, pair):
-            h_rows(c, [2 * pair, 2 * pair + 1], take_h_bank(), h_sb[pair][:, :, c * CH : (c + 1) * CH])
+        def make_h(c, pair, bank=None):
+            h_rows(c, [2 * pair, 2 * pair + 1], take_h_bank() if bank is None else bank, h_sb[pair][:, :, c * CH : (c + 1) * CH])
 
         def put_rows(c, t, count=1):
             first, width = c * CH, count * CH
-            half, at = divmod(first, S // 2)
+            held = max(a for tile, a in wgs_sb if tile == t and a <= first)
+            at = first - held
             nc.vector.tensor_tensor(
                 out=page[t][:].indirect(list2[:, first // 16 : (first + width) // 16]),
                 in0=h_sb[t // 2][:, t % 2, first : first + width],
-                in1=wgs_sb[t, half][:, at : at + width],
+                in1=wgs_sb[t, held][:, at : at + width],
                 op=ALU.mult,
             )
 
@@ -327,7 +331,8 @@ def tile_list_fellow_eye_fitting_kernel(
             )
 
         out_rows = out.rearrange("(p t) j -> p t j", t=4)
-        x_bf = [kept(f"x_bf{q}", [P, QW * 4], BF16) for q in range(PN // QW)]
+        pieces = [slice(a, b) for a, b in PIECES]
+        x_bf = [kept(f"x_bf{q}", [P, (cols.stop - cols.start) * 4], BF16) for q, cols in enumerate(pieces)]
         take_turns = ring("turns", TURN_RING, [P, PN], F32)
         take_whole = ring("whole", WHOLE_RING, [P, PN], U32)
         take_rest = ring("rest", REST_RING, [P, PN], F32)
@@ -398,68 +403,80 @@ def tile_list_fellow_eye_fitting_kernel(
         def weave(q):
             nc.scalar.copy(
                 out=x_bf[q][:].rearrange("p (j t) -> p j t", t=4)[:, :, 0:3],
-                in_=x_rows[:, :, q * QW : (q + 1) * QW].rearrange("p t j -> p j t"),
+                in_=x_rows[:, :, pieces[q]].rearrange("p t j -> p j t"),
             )
 
         def scale_last(q):
             nc.vector.tensor_scalar(
-                out=x_bf[q][:].rearrange("p (j t) -> p t j", t=4)[:, 3, :], in0=rest[3][:, q * QW : (q + 1) * QW],
+                out=x_bf[q][:].rearrange("p (j t) -> p t j", t=4)[:, 3, :], in0=rest[3][:, pieces[q]],
                 scalar1=gain_sb[:, 3:4], scalar2=None, op0=ALU.mult,
             )
 
         take_y_bank = bank_ring(Y_BANKS)
-        take_x_w = ring("x_w", 2, [P, QW], U32)
-        take_x_s = ring("x_s", 2, [P, QW], U8)
-        take_y = ring("y_sb", Y_RING, [P, QW], F32)
-        take_result = ring("result", RES_RING, [P, 2, QW], F32)
-        accs = {}
+        take_y = ring("y_sb", Y_RING, [P, HW], F32)
+        spare = [raw[:, j, :] for raw in w1_raw + w3_raw for j in range(4)]
+        stored = []
+
+        def take_result():
+            stored.append(0)
+            return spare[len(stored) - 1]
+
+        sums = {}
 
         def last_product(q):
-            x_w = take_x_w()
-            x_s = take_x_s()
+            width = pieces[q].stop - pieces[q].start
+            x_w = kept(f"x_w{q}", [P, width], U32)
+            x_s = kept(f"x_s{q}", [P, width], U8)
             quantise(x_bf[q][:], x_w[:], x_s[:])
-            for pair in range(2):
-                acc = take_y_bank()
-                accs[q, pair] = acc
-                for i in range(2):
-                    t = 2 * pair + i
-                    nc.tensor.matmul_mx(
-                        out=acc[:, QW * i : QW * (i + 1)],
-                        lhsT=w4_w[:, 128 * t : 128 * (t + 1)].bitcast(FP8X4),
-                        lhsT_scale=w4_s[:, 128 * t : 128 * (t + 1)],
-                        rhs=x_w[:].bitcast(FP8X4),
-                        rhs_scale=x_s[:],
-                        start=True,
-                        stop=True,
-                    )
+            for t in range(4):
+                if t * width % HW == 0:
+                    bank = take_y_bank()
+                sums[q, t] = bank[:, t * width % HW : t * width % HW + width]
+                nc.tensor.matmul_mx(
+                    out=sums[q, t],
+                    lhsT=w4_w[:, 128 * t : 128 * (t + 1)].bitcast(FP8X4),
+                    lhsT_scale=w4_s[:, 128 * t : 128 * (t + 1)],
+                    rhs=x_w[:].bitcast(FP8X4),
+                    rhs_scale=x_s[:],
+                    start=True,
+                    stop=True,
+                )
 
         def finish(q):
-            picks = list4[:, q * QW // 16 : (q + 1) * QW // 16]
-            for pair in range(2):
-                result = take_result()
-                for i in range(2):
-                    t = 2 * pair + i
-                    y_sb = take_y()
-                    nc.scalar.activation(
-                        out=y_sb[:], in_=accs[q, pair][:, QW * i : QW * (i + 1)], func=ACT.Identity, bias=base_sb[:, t : t + 1]
+            cols = pieces[q]
+            width = cols.stop - cols.start
+            rows = HW // width
+            for t in range(4):
+                if t % rows == 0:
+                    result = take_result()
+                y_sb = take_y()
+                nc.scalar.activation(out=y_sb[:, 0:width], in_=sums[q, t], func=ACT.Identity, bias=base_sb[:, t : t + 1])
+                nc.vector.tensor_tensor(
+                    out=result[:, t % rows * width : (t % rows + 1) * width],
+                    in0=page[t][:].indirect(list4[:, cols.start // 16 : cols.stop // 16]),
+                    in1=y_sb[:, 0:width],
+                    op=ALU.mult,
+                )
+                if t % rows == rows - 1:
+                    nc.sync.dma_start(
+                        out=out_rows[:, t + 1 - rows : t + 1, cols], in_=result.rearrange("p (i j) -> p i j", i=rows)
                     )
-                    nc.vector.tensor_tensor(out=result[:, i, :], in0=page[t][:].indirect(picks), in1=y_sb[:], op=ALU.mult)
-                nc.sync.dma_start(out=out_rows[:, 2 * pair : 2 * pair + 2, q * QW : (q + 1) * QW], in_=result[:])
 
         last = NCH - 1
         halves = [slice(0, HW), slice(HW, PN)]
         quarters = [slice(q * QW, (q + 1) * QW) for q in range(4)]
         make_h(last, 0)
-        for c in range(NCH):
-            make_h(c, 1)
+        for c in range(last):
+            make_h(c, 1, take_irr())
+        make_h(last, 1)
         for t in range(4):
             if t < 2:
                 put_rows(last, t)
-                load_wgs(2, t, wgs_sb[t, 1])
+                load_wgs(2, t * 2 * CH, 2 * CH, wgs_tiles[2 + t])
             elif t == 2:
                 for half in range(2):
                     put_rows(2 * half, 2, 2)
-                    load_wgs(3, half, wgs_sb[2, half])
+                    load_wgs(3, half * 1 * CH, (NCH - 1 if half else 1) * CH, wgs_tiles[2 + half])
             if t < 3:
                 pick(t)
                 for cols in halves:
@@ -478,10 +495,10 @@ def tile_list_fellow_eye_fitting_kernel(
                 for cols in halves:
                     sine_turned(t, cols)
                 scale_back(t, halves[0])
-        for q in range(4):
+        for q in range(len(pieces)):
             weave(q)
-        put_rows(0, 3, 2)
-        put_rows(2, 3, 2)
+        put_rows(0, 3, 1)
+        put_rows(1, 3, NCH - 1)
         deal_w4()
         pick(3)
         round_turns(3, quarters[0])
@@ -496,12 +513,8 @@ def tile_list_fellow_eye_fitting_kernel(
         sine(3, quarters[1])
         scale_last(1)
         last_product(1)
-        finish(0)
         sine(3, halves[1])
         scale_last(2)
-        scale_last(3)
-        finish(1)
         last_product(2)
-        last_product(3)
-        finish(2)
-        finish(3)
+        for q in range(len(pieces)):
+            finish(q)

@@ -4,7 +4,9 @@ from contextlib import ExitStack
 import concourse.mybir as mybir
 from concourse.masks import make_identity
 
-K, M, H, T, S, T2, PN = 512, 1024, 512, 2048, 1024, 2048, 1024
+K, M, H = 512, 1024, 512
+T, T2 = 2048, 2048
+S, PN = 1024, 1024
 FLOPS = 2 * (2 * K * M * S + M * H * S + H * H * PN)
 
 F32 = mybir.dt.float32
@@ -19,35 +21,19 @@ ALU = mybir.AluOpType
 ACT = mybir.ActivationFunctionType
 
 P = 128
-CH = 256
-NCH = S // CH
-UW = 128
-HW = 512
-QW = 256
+PACK = 4
+PASS = P * PACK
+BANK = 512
+STRIPE = 16
+CHUNK = 256
+CHUNKS = S // CHUNK
+UNIT = BANK // PACK
+HALVES = [slice(0, PN // 2), slice(PN // 2, PN)]
+PIECES = [slice(0, 256), slice(256, 512), slice(512, PN)]
+TABLE_AHEAD = 3
+DAMP_AHEAD = 6
+ON_TENSOR = (0, 1)
 ROUNDER = 12582912.0
-SMALL_AFTER = 1
-V_RING = 3
-IRR_BANKS = [0,1,2]
-CURV_BANKS = [3,4,7]
-EARLY_BANKS = [5]
-LATE_BANKS = [6,7]
-Y_BANKS = [0,1,2,3,4,5,6,7]
-DAMP_RING = 6
-EARLY_RING = 4
-HAND_RING = 2
-TURN_RING = 2
-REST_RING = 2
-Y_RING = 4
-RES_RING = 4
-CASTS = "vvvv"
-GAIN_ON_VECTOR = ((3, 0), (3, 1))
-WHOLE_RING = 2
-SIN_WARM = 1
-H_BANKS = [5,6]
-T_BANKS = [3,4]
-B_BANKS = [7,0]
-M_RING = 2
-PIECES = [[0,256],[256,512],[512,1024]]
 
 
 def tile_list_fellow_eye_fitting_kernel(
@@ -63,26 +49,35 @@ def tile_list_fellow_eye_fitting_kernel(
         def kept(name, shape, dtype):
             return keep.tile(shape, dtype, name=name, align_bytes=64)
 
+        def in_turn(members):
+            taken = []
+
+            def take():
+                taken.append(None)
+                return members[(len(taken) - 1) % len(members)]
+
+            return take
+
         def ring(name, count, shape, dtype):
-            tiles = [kept(f"{name}{i}", shape, dtype) for i in range(count)]
-            turn = []
+            return in_turn([kept(f"{name}{i}", shape, dtype) for i in range(count)])
 
-            def take():
-                turn.append(0)
-                return tiles[(len(turn) - 1) % count]
+        def entries(list_tile, cols):
+            return list_tile[:, cols.start // STRIPE : cols.stop // STRIPE]
 
-            return take
+        def quantise(values_bf, name):
+            width = values_bf.shape[1] // PACK
+            codes = kept(name + "_codes", [P, width], U32)
+            plane = kept(name + "_plane", [P, width], U8)
+            nc.vector.quantize_mx(out=codes[:].bitcast(FP8X4), scales=plane[:], in_=values_bf)
+            return codes, plane
 
-        banks = [psum.tile([P, 512], F32, name=f"bank{i}") for i in range(8)]
-
-        def bank_ring(members):
-            turn = []
-
-            def take():
-                turn.append(0)
-                return banks[members[(len(turn) - 1) % len(members)]]
-
-            return take
+        banks = [psum.tile([P, BANK], F32, name=f"bank{i}") for i in range(8)]
+        take_irr_bank = in_turn(banks[0:3])
+        take_curv_bank = in_turn([banks[3], banks[4], banks[7]])
+        take_h_bank = in_turn(banks[5:7])
+        take_turned_bank = in_turn(banks[3:5])
+        take_back_bank = in_turn([banks[7], banks[0]])
+        take_y_bank = in_turn(banks)
 
         def load_list(name, src):
             tile = lists.tile([P, src.shape[1]], U16, name=name)
@@ -94,427 +89,389 @@ def tile_list_fellow_eye_fitting_kernel(
             nc.vector.memset(plane[:].bitcast(I32), 0)
             return plane
 
-        def load_plane(plane, src, queue):
+        def load_scale_rows(plane, src):
             for quad in range(4):
-                queue.dma_start(
+                nc.sync.dma_start(
                     out=plane[32 * quad : 32 * quad + 4, :].bitcast(I32),
                     in_=src[0, 4 * quad : 4 * quad + 4, :].bitcast(I32),
                 )
 
-        tab_s = zeroed_plane("tab_s", T)
-        w2_s_plane = zeroed_plane("w2_s_plane", M)
-        w4_s_raw = zeroed_plane("w4_s_raw", H)
-
-        list1 = load_list("list1", offs)
-        w2_s_raw = kept("w2_s_raw", [P, M], U8)
-        load_plane(w2_s_raw, w2_scales, nc.sync)
-        w2_raw = kept("w2_raw", [P, M // 2], I32)
-        nc.sync.dma_start(out=w2_raw[:], in_=w2_words[0].bitcast(I32))
-        tab_w = kept("tab_w", [P, T], I32)
-        nc.sync.dma_start(out=tab_w[:], in_=tab_words[0].rearrange("p t i -> p (t i)").bitcast(I32))
-        load_plane(tab_s, tab_scales, nc.sync)
-        warm = kept("warm", [P, 4], F32)
-        nc.vector.memset(warm[:, 0:1], 1.0)
-        nc.scalar.activation(out=warm[:, 1:2], in_=warm[:, 0:1], func=ACT.Abs_reciprocal_sqrt)
-        w1_raw = [kept(f"w1_raw{b}", [P, 4, 512], F32) for b in range(2)]
-        w3_raw = [kept(f"w3_raw{b}", [P, 4, 512], F32) for b in range(2)]
-        for b in range(2):
-            nc.sync.dma_start(out=w1_raw[b][:], in_=w1[:, 512 * b : 512 * (b + 1)].rearrange("(p j) m -> p j m", j=4))
-        for b in range(2):
-            nc.sync.dma_start(out=w3_raw[b][:], in_=w3[512 * b : 512 * (b + 1), :].rearrange("(p j) r -> p j r", j=4))
-        list2 = load_list("list2", offs2)
-        wgs_rows = wgs.rearrange("(q t) j -> q t j", t=4)
-        wgs_sb = {}
-        page_rows = page0.rearrange("(p t) c -> p t c", t=4)
-        page = [kept(f"page{t}", [P, T2], F32) for t in range(4)]
-
-        def load_wgs(t, first, width, into):
-            wgs_sb[t, first] = into
-            for quad in range(4):
-                nc.sync.dma_start(out=into[32 * quad : 32 * (quad + 1), 0:width], in_=wgs_rows[:, t, first : first + width])
-
-        wgs_tiles = [kept(f"wgs{i}", [P, 3 * CH if i == 3 else 2 * CH], F32) for i in range(4)]
-
-        def load_page(t):
-            nc.sync.dma_start(out=page[t][:], in_=page_rows[:, t, :])
-
         def load_column(name, vec):
-            tile = kept(name, [P, 4], F32)
-            nc.sync.dma_start(out=tile[:], in_=vec.rearrange("(p t) -> p t", t=4))
+            tile = kept(name, [P, PACK], F32)
+            nc.sync.dma_start(out=tile[:], in_=vec.rearrange("(p t) -> p t", t=PACK))
             return tile
 
-        def load_w4():
-            raw = kept("w4_raw", [P, H], I32)
-            nc.sync.dma_start(out=raw[:], in_=w4_words[0].rearrange("p c i -> p (c i)").bitcast(I32))
-            load_plane(w4_s_raw, w4_scales, nc.sync)
-            return raw
+        tab_plane = zeroed_plane("tab_plane", T)
+        w2_plane_raw = zeroed_plane("w2_plane_raw", M)
+        w4_plane_raw = zeroed_plane("w4_plane_raw", H)
 
+        list1 = load_list("list1", offs)
+        w2_rows = kept("w2_rows", [P, M], U8)
+        load_scale_rows(w2_rows, w2_scales)
+        w2_raw = kept("w2_raw", [P, M // 2], I32)
+        nc.sync.dma_start(out=w2_raw[:], in_=w2_words[0].bitcast(I32))
+        tab_codes = kept("tab_codes", [P, T], I32)
+        nc.sync.dma_start(out=tab_codes[:], in_=tab_words[0].rearrange("p t i -> p (t i)").bitcast(I32))
+        load_scale_rows(tab_plane, tab_scales)
+        w1_raw = [kept(f"w1_raw{b}", [P, PACK, PASS], F32) for b in range(2)]
+        w3_raw = [kept(f"w3_raw{b}", [P, PACK, H], F32) for b in range(2)]
+        for b in range(2):
+            nc.sync.dma_start(
+                out=w1_raw[b][:], in_=w1[:, PASS * b : PASS * (b + 1)].rearrange("(p i) m -> p i m", i=PACK)
+            )
+        for b in range(2):
+            nc.sync.dma_start(
+                out=w3_raw[b][:], in_=w3[PASS * b : PASS * (b + 1), :].rearrange("(p i) r -> p i r", i=PACK)
+            )
+        list2 = load_list("list2", offs2)
+
+        wgs_rows = wgs.rearrange("(q t) j -> q t j", t=PACK)
+        wgs_tiles = [kept(f"wgs{i}", [P, (3 if i == 3 else 2) * CHUNK], F32) for i in range(4)]
+        wgs_held = {}
+
+        def load_wgs(t, chunks, tile):
+            for c in chunks:
+                wgs_held[t, c] = (tile, (c - chunks.start) * CHUNK)
+            for quad in range(4):
+                nc.sync.dma_start(
+                    out=tile[32 * quad : 32 * (quad + 1), 0 : len(chunks) * CHUNK],
+                    in_=wgs_rows[:, t, chunks.start * CHUNK : chunks.stop * CHUNK],
+                )
+
+        page_rows = page0.rearrange("(p t) c -> p t c", t=PACK)
+        page = [kept(f"page{t}", [P, T2], F32) for t in range(PACK)]
+        chunk_pairs = [range(0, 2), range(2, 4)]
         for t in range(2):
-            load_wgs(t, 0, 2 * CH, wgs_tiles[t])
-            load_page(t)
+            load_wgs(t, chunk_pairs[0], wgs_tiles[t])
+            nc.sync.dma_start(out=page[t][:], in_=page_rows[:, t, :])
         for t in range(2):
-            load_wgs(t, 2 * CH, 2 * CH, wgs_tiles[2 + t])
-        w4_raw = load_w4()
+            load_wgs(t, chunk_pairs[1], wgs_tiles[2 + t])
+        w4_raw = kept("w4_raw", [P, H], I32)
+        nc.sync.dma_start(out=w4_raw[:], in_=w4_words[0].rearrange("p c i -> p (c i)").bitcast(I32))
+        load_scale_rows(w4_plane_raw, w4_scales)
         list3 = load_list("list3", offs3)
         gain_sb = load_column("gain_sb", gain)
-        load_page(2)
-        load_page(3)
+        for t in range(2, PACK):
+            nc.sync.dma_start(out=page[t][:], in_=page_rows[:, t, :])
         list4 = load_list("list4", offs4)
         base_sb = load_column("base_sb", base)
 
-        v_w = {}
-        v_s = {}
-        take_v_w = ring("v_w", V_RING, [P, CH], U32)
-        take_v_s = ring("v_s", V_RING, [P, CH], U8)
+        def deal(dst, src):
+            nc.vector.tensor_copy(
+                out=dst.rearrange("p (t q) -> p q t", t=PACK), in_=src.rearrange("p (q t) -> p q t", t=PACK)
+            )
 
-        def gather_table(c):
-            v_w[c] = take_v_w()
-            v_s[c] = take_v_s()
-            picks = list1[:, c * CH // 16 : (c + 1) * CH // 16]
-            nc.vector.tensor_copy(out=v_w[c][:], in_=tab_w[:].bitcast(U32).indirect(picks))
-            nc.vector.tensor_copy(out=v_s[c][:], in_=tab_s[:].indirect(picks))
-
-        w2_w = kept("w2_w", [P, 2 * M], U8)
-        w2_s = kept("w2_s", [P, M], U8)
+        w2_codes = kept("w2_codes", [P, 2 * M], U8)
+        w2_plane = kept("w2_plane", [P, M], U8)
         for quad in range(4):
             live = slice(32 * quad, 32 * quad + 4)
-            nc.vector.tensor_copy(out=w2_s_plane[live, :].bitcast(I32), in_=w2_s_raw[live, :].bitcast(I32))
+            nc.vector.tensor_copy(out=w2_plane_raw[live, :].bitcast(I32), in_=w2_rows[live, :].bitcast(I32))
         for b in range(2):
+            cols = slice(PASS * b, PASS * (b + 1))
+            deal(w2_plane[:, cols], w2_plane_raw[:, cols])
+            deal(w2_codes[:].bitcast(U16)[:, cols], w2_raw[:].bitcast(U16)[:, cols])
+
+        take_v_codes = ring("v_codes", TABLE_AHEAD, [P, CHUNK], U32)
+        take_v_plane = ring("v_plane", TABLE_AHEAD, [P, CHUNK], U8)
+        v_codes = {}
+        v_plane = {}
+
+        def gather_table(c):
+            v_codes[c] = take_v_codes()
+            v_plane[c] = take_v_plane()
+            picks = entries(list1, slice(c * CHUNK, (c + 1) * CHUNK))
+            nc.vector.tensor_copy(out=v_codes[c][:], in_=tab_codes[:].bitcast(U32).indirect(picks))
+            nc.vector.tensor_copy(out=v_plane[c][:], in_=tab_plane[:].indirect(picks))
+
+        take_weight_bf = ring("weight_bf", 2, [P, PASS * PACK], BF16)
+
+        def quantise_weight(name, raw):
+            weight_bf = take_weight_bf()
             nc.vector.tensor_copy(
-                out=w2_s[:, 512 * b : 512 * (b + 1)].rearrange("p (t q) -> p q t", t=4),
-                in_=w2_s_plane[:, 512 * b : 512 * (b + 1)].rearrange("p (q t) -> p q t", t=4),
+                out=weight_bf[:].rearrange("p (t q i) -> p q i t", t=PACK, i=PACK),
+                in_=raw[:].rearrange("p i (q t) -> p q i t", t=PACK),
             )
-            nc.vector.tensor_copy(
-                out=w2_w[:].bitcast(U16)[:, 512 * b : 512 * (b + 1)].rearrange("p (t q) -> p q t", t=4),
-                in_=w2_raw[:].bitcast(U16)[:, 512 * b : 512 * (b + 1)].rearrange("p (q t) -> p q t", t=4),
-            )
+            return quantise(weight_bf[:], name)
 
-        def quantise(src_bf, codes, scales):
-            nc.vector.quantize_mx(out=codes.bitcast(FP8X4), scales=scales, in_=src_bf)
-
-        take_w_bf = ring("w_bf", 2, [P, 2048], BF16)
-
-        def prepare_weight(name, raw, copy):
-            grouped = take_w_bf()
-            copy(
-                out=grouped[:].rearrange("p (t q j) -> p q t j", t=4, j=4),
-                in_=raw[:].rearrange("p j (q t) -> p q t j", t=4),
-            )
-            codes = kept(name + "_w", [P, 512], U32)
-            scales = kept(name + "_s", [P, 512], U8)
-            quantise(grouped[:], codes[:], scales[:])
-            return codes, scales
-
+        take_damp = ring("damp", DAMP_AHEAD, [P, BANK], F32)
+        take_ratio_bf = ring("ratio_bf", 2, [P, 2 * CHUNK * PACK], BF16)
         w1_q = {}
         w3_q = {}
-        ratio_w = {}
-        ratio_s = {}
-        take_irr = bank_ring(IRR_BANKS)
-        take_curv = bank_ring(CURV_BANKS)
-        take_damp = ring("damp", DAMP_RING, [P, UW * 4], F32)
-        take_ratio_bf = ring("ratio_bf", 2, [P, 2 * CH * 4], BF16)
         ratio_bf = {}
+        ratio_q = {}
+
+        def row_tiles(bank, weight_codes, weight_plane, c, cols):
+            for t in range(PACK):
+                nc.tensor.matmul_mx(
+                    out=bank[:, UNIT * t : UNIT * (t + 1)],
+                    lhsT=weight_codes(t),
+                    lhsT_scale=weight_plane[:, P * t : P * (t + 1)],
+                    rhs=v_codes[c][:, cols].bitcast(FP8X4),
+                    rhs_scale=v_plane[c][:, cols],
+                    start=True,
+                    stop=True,
+                )
 
         def ratio_pass(c, b):
-            damp = []
-            for u in range(CH // UW):
-                cols = slice(u * UW, (u + 1) * UW)
-                irr = take_irr()
-                for t in range(4):
-                    col = 512 * b + 128 * t
-                    nc.tensor.matmul_mx(
-                        out=irr[:, UW * t : UW * (t + 1)],
-                        lhsT=w2_w[:, 2 * col : 2 * (col + 128)].bitcast(FP4X4),
-                        lhsT_scale=w2_s[:, col : col + 128],
-                        rhs=v_w[c][:, cols].bitcast(FP8X4),
-                        rhs_scale=v_s[c][:, cols],
-                        start=True,
-                        stop=True,
-                    )
-                d = take_damp()
+            units = [slice(first, first + UNIT) for first in range(0, CHUNK, UNIT)]
+            damps = []
+            for cols in units:
+                irr = take_irr_bank()
+                row_tiles(
+                    irr,
+                    lambda t: w2_codes[:, 2 * (PASS * b + P * t) : 2 * (PASS * b + P * (t + 1))].bitcast(FP4X4),
+                    w2_plane[:, PASS * b : PASS * (b + 1)],
+                    c,
+                    cols,
+                )
+                damp = take_damp()
                 nc.scalar.activation(
-                    out=d[:].rearrange("p (j t) -> p j t", t=4),
-                    in_=irr[:].rearrange("p (t j) -> p j t", t=4),
+                    out=damp[:].rearrange("p (j t) -> p j t", t=PACK),
+                    in_=irr[:].rearrange("p (t j) -> p j t", t=PACK),
                     func=ACT.Abs,
                 )
-                damp.append(d)
-            for d in damp:
-                nc.scalar.activation(out=d[:], in_=d[:], func=ACT.Abs_reciprocal_sqrt, bias=1.0)
-            for d in damp:
-                nc.scalar.activation(out=d[:], in_=d[:], func=ACT.Square)
-            if (c, b) == (NCH - 1, 1) and SIN_WARM:
-                nc.scalar.activation(out=warm[:, 2:3], in_=damp[-1][:, 0:1], func=ACT.Sin)
+                damps.append(damp)
+            for damp in damps:
+                nc.scalar.activation(out=damp[:], in_=damp[:], func=ACT.Abs_reciprocal_sqrt, bias=1.0)
+            for damp in damps:
+                nc.scalar.activation(out=damp[:], in_=damp[:], func=ACT.Square)
             if b == 0:
                 ratio_bf[c] = take_ratio_bf()
-            for u in range(CH // UW):
-                cols = slice(u * UW, (u + 1) * UW)
-                curv = take_curv()
-                for t in range(4):
-                    nc.tensor.matmul_mx(
-                        out=curv[:, UW * t : UW * (t + 1)],
-                        lhsT=w1_q[b][0][:, 128 * t : 128 * (t + 1)].bitcast(FP8X4),
-                        lhsT_scale=w1_q[b][1][:, 128 * t : 128 * (t + 1)],
-                        rhs=v_w[c][:, cols].bitcast(FP8X4),
-                        rhs_scale=v_s[c][:, cols],
-                        start=True,
-                        stop=True,
-                    )
+            for cols, damp in zip(units, damps):
+                curv = take_curv_bank()
+                row_tiles(curv, lambda t: w1_q[b][0][:, P * t : P * (t + 1)].bitcast(FP8X4), w1_q[b][1], c, cols)
+                words = slice((b * CHUNK + cols.start) * PACK, (b * CHUNK + cols.stop) * PACK)
                 nc.vector.tensor_tensor(
-                    out=ratio_bf[c][:, (b * CH + u * UW) * 4 : (b * CH + (u + 1) * UW) * 4].rearrange("p (j t) -> p j t", t=4),
-                    in0=curv[:].rearrange("p (t j) -> p j t", t=4),
-                    in1=damp[u][:].rearrange("p (j t) -> p j t", t=4),
+                    out=ratio_bf[c][:, words].rearrange("p (j t) -> p j t", t=PACK),
+                    in0=curv[:].rearrange("p (t j) -> p j t", t=PACK),
+                    in1=damp[:].rearrange("p (j t) -> p j t", t=PACK),
                     op=ALU.mult,
                 )
             if b == 1:
-                ratio_w[c] = kept(f"ratio_w{c}", [P, 2 * CH], U32)
-                ratio_s[c] = kept(f"ratio_s{c}", [P, 2 * CH], U8)
-                quantise(ratio_bf[c][:], ratio_w[c][:], ratio_s[c][:])
+                ratio_q[c] = quantise(ratio_bf[c][:], f"ratio{c}")
 
-        def h_rows(c, tiles, acc, dst):
-            for i, t in enumerate(tiles):
+        h_sb = [kept(f"h{pair}", [P, 2, S], F32) for pair in range(2)]
+
+        def make_h(c, pair, bank):
+            codes, plane = ratio_q[c]
+            for i in range(2):
+                t = 2 * pair + i
                 for b in range(2):
                     nc.tensor.matmul_mx(
-                        out=acc[:, CH * i : CH * (i + 1)],
-                        lhsT=w3_q[b][0][:, 128 * t : 128 * (t + 1)].bitcast(FP8X4),
-                        lhsT_scale=w3_q[b][1][:, 128 * t : 128 * (t + 1)],
-                        rhs=ratio_w[c][:, b * CH : (b + 1) * CH].bitcast(FP8X4),
-                        rhs_scale=ratio_s[c][:, b * CH : (b + 1) * CH],
+                        out=bank[:, CHUNK * i : CHUNK * (i + 1)],
+                        lhsT=w3_q[b][0][:, P * t : P * (t + 1)].bitcast(FP8X4),
+                        lhsT_scale=w3_q[b][1][:, P * t : P * (t + 1)],
+                        rhs=codes[:, b * CHUNK : (b + 1) * CHUNK].bitcast(FP8X4),
+                        rhs_scale=plane[:, b * CHUNK : (b + 1) * CHUNK],
                         start=(b == 0),
                         stop=(b == 1),
                     )
-            nc.scalar.copy(out=dst, in_=acc[:].rearrange("p (i j) -> p i j", i=2))
+            nc.scalar.copy(
+                out=h_sb[pair][:, :, c * CHUNK : (c + 1) * CHUNK], in_=bank[:].rearrange("p (i j) -> p i j", i=2)
+            )
 
-        take_h_bank = bank_ring(H_BANKS)
-        h_sb = [kept(f"h{pair}", [P, 2, S], F32) for pair in range(2)]
-
-        def make_h(c, pair, bank=None):
-            h_rows(c, [2 * pair, 2 * pair + 1], take_h_bank() if bank is None else bank, h_sb[pair][:, :, c * CH : (c + 1) * CH])
-
-        def put_rows(c, t, count=1):
-            first, width = c * CH, count * CH
-            held = max(a for tile, a in wgs_sb if tile == t and a <= first)
-            at = first - held
+        def put(t, chunks):
+            cols = slice(chunks.start * CHUNK, chunks.stop * CHUNK)
+            wgs_tile, at = wgs_held[t, chunks.start]
             nc.vector.tensor_tensor(
-                out=page[t][:].indirect(list2[:, first // 16 : (first + width) // 16]),
-                in0=h_sb[t // 2][:, t % 2, first : first + width],
-                in1=wgs_sb[t, held][:, at : at + width],
+                out=page[t][:].indirect(entries(list2, cols)),
+                in0=h_sb[t // 2][:, t % 2, cols],
+                in1=wgs_tile[:, at : at + len(chunks) * CHUNK],
                 op=ALU.mult,
             )
 
-        vcopy, scopy = nc.vector.tensor_copy, nc.scalar.copy
         gather_table(0)
-        w1_q[0] = prepare_weight("w1_0", w1_raw[0], CASTS[0] == "v" and vcopy or scopy)
+        w1_q[0] = quantise_weight("w1_0", w1_raw[0])
         ratio_pass(0, 0)
-        w1_q[1] = prepare_weight("w1_1", w1_raw[1], CASTS[1] == "v" and vcopy or scopy)
+        w1_q[1] = quantise_weight("w1_1", w1_raw[1])
         gather_table(1)
         ratio_pass(0, 1)
-        w3_q[0] = prepare_weight("w3_0", w3_raw[0], CASTS[2] == "v" and vcopy or scopy)
-        w3_q[1] = prepare_weight("w3_1", w3_raw[1], CASTS[3] == "v" and vcopy or scopy)
-        for c in range(NCH - 1):
-            if c + 2 < NCH:
+        for b in range(2):
+            w3_q[b] = quantise_weight(f"w3_{b}", w3_raw[b])
+        last = CHUNKS - 1
+        for c in range(last):
+            if c + 2 < CHUNKS:
                 gather_table(c + 2)
             ratio_pass(c + 1, 0)
             ratio_pass(c + 1, 1)
-            make_h(c, 0)
+            make_h(c, 0, take_h_bank())
             for t in range(2):
-                put_rows(c, t)
+                put(t, range(c, c + 1))
 
-        w4_w = kept("w4_w", [P, H], I32)
-        w4_s = kept("w4_s", [P, H], U8)
-
-        def deal_w4():
-            nc.vector.tensor_copy(
-                out=w4_w[:].rearrange("p (t q) -> p q t", t=4), in_=w4_raw[:].rearrange("p (q t) -> p q t", t=4)
-            )
-            nc.vector.tensor_copy(
-                out=w4_s[:].rearrange("p (t q) -> p q t", t=4), in_=w4_s_raw[:].rearrange("p (q t) -> p q t", t=4)
-            )
-
-        out_rows = out.rearrange("(p t) j -> p t j", t=4)
-        pieces = [slice(a, b) for a, b in PIECES]
-        x_bf = [kept(f"x_bf{q}", [P, (cols.stop - cols.start) * 4], BF16) for q, cols in enumerate(pieces)]
-        take_turns = ring("turns", TURN_RING, [P, PN], F32)
-        take_whole = ring("whole", WHOLE_RING, [P, PN], U32)
-        take_rest = ring("rest", REST_RING, [P, PN], F32)
-        x_rows = kept("x_rows", [P, 3, PN], BF16)
+        w4_codes = kept("w4_codes", [P, H], I32)
+        w4_plane = kept("w4_plane", [P, H], U8)
+        x_bf = [kept(f"x_bf{q}", [P, (cols.stop - cols.start) * PACK], BF16) for q, cols in enumerate(PIECES)]
+        take_turns = ring("turns", 2, [P, PN], F32)
+        take_whole = ring("whole", 2, [P, PN], U32)
+        rest = {t: kept(f"rest{t}", [P, PN], F32) for t in range(PACK) if t not in ON_TENSOR}
+        x_rows = kept("x_rows", [P, PACK - 1, PN], BF16)
+        identity = kept("identity", [P, P], F32)
+        make_identity(nc, identity[:])
+        take_minus_whole = ring("minus_whole", 2, [P, BANK], F32)
+        take_sine_turned = ring("sine_turned", 2, [P, BANK], F32)
         turns = {}
         whole = {}
-        rest = {}
+        minus_whole = {}
+        sine_turned = {}
 
-        def pick(t):
+        def pick_turns(t):
             turns[t] = take_turns()
             whole[t] = take_whole()
-            rest[t] = take_rest()
-            for a in range(0, PN, HW):
+            for cols in HALVES:
                 nc.vector.tensor_scalar(
-                    out=turns[t][:, a : a + HW], in0=page[t][:].indirect(list3[:, a // 16 : (a + HW) // 16]),
+                    out=turns[t][:, cols], in0=page[t][:].indirect(entries(list3, cols)),
                     scalar1=1.0 / (2.0 * math.pi), scalar2=0.0, op0=ALU.mult, op1=ALU.add,
                 )
 
         def round_turns(t, cols):
             nc.scalar.activation(out=whole[t][:, cols], in_=turns[t][:, cols], func=ACT.Copy, bias=ROUNDER)
 
-        def reduce(t, cols):
+        def reduce_on_vector(t, cols):
             nc.vector.scalar_tensor_tensor(
                 out=rest[t][:, cols], in0=whole[t][:, cols].bitcast(I32), scalar=ROUNDER, in1=turns[t][:, cols],
                 op0=ALU.subtract, op1=ALU.subtract,
             )
 
-        def sine(t, cols):
+        def sine_of_rest(t, cols):
             nc.scalar.activation(out=rest[t][:, cols], in_=rest[t][:, cols], func=ACT.Sin, scale=-2.0 * math.pi)
 
-        identity = kept("identity", [P, P], F32)
-        make_identity(nc, identity[:])
-        take_turn_bank = bank_ring(T_BANKS)
-        take_back_bank = bank_ring(B_BANKS)
-        take_minus = ring("minus_whole", M_RING, [P, HW], F32)
-        take_sine = ring("sine_t", M_RING, [P, HW], F32)
-        minus = {}
-        sine_t = {}
+        def scale_row(t, cols, sine):
+            nc.scalar.activation(out=x_rows[:, t, cols], in_=sine, func=ACT.Copy, scale=gain_sb[:, t : t + 1])
 
-        def negate(t, cols):
-            minus[t, cols.start] = take_minus()
-            nc.scalar.activation(out=minus[t, cols.start][:], in_=whole[t][:, cols], func=ACT.Copy, scale=-1.0, bias=ROUNDER)
+        def negate_whole(t, cols):
+            minus_whole[t, cols.start] = take_minus_whole()
+            nc.scalar.activation(
+                out=minus_whole[t, cols.start][:], in_=whole[t][:, cols], func=ACT.Copy, scale=-1.0, bias=ROUNDER
+            )
 
-        def sine_turned(t, cols):
-            bank = take_turn_bank()
-            for a in range(0, HW, P):
-                nc.tensor.matmul(
-                    out=bank[:, a : a + P], lhsT=turns[t][:, cols.start + a : cols.start + a + P], rhs=identity[:],
-                    start=(a == 0), stop=False, is_transpose=True,
-                )
-            for a in range(0, HW, P):
-                nc.tensor.matmul(
-                    out=bank[:, a : a + P], lhsT=minus[t, cols.start][:, a : a + P], rhs=identity[:],
-                    start=False, stop=(a == HW - P), is_transpose=True,
-                )
-            sine_t[t, cols.start] = take_sine()
-            nc.scalar.activation(out=sine_t[t, cols.start][:], in_=bank[:], func=ACT.Sin, scale=2.0 * math.pi)
+        def sine_on_tensor(t, cols):
+            bank = take_turned_bank()
+            terms = [turns[t][:, cols], minus_whole[t, cols.start][:]]
+            for n, term in enumerate(terms):
+                for a in range(0, BANK, P):
+                    nc.tensor.matmul(
+                        out=bank[:, a : a + P], lhsT=term[:, a : a + P], rhs=identity[:],
+                        start=(n == 0 and a == 0), stop=(n == 1 and a == BANK - P), is_transpose=True,
+                    )
+            sine_turned[t, cols.start] = take_sine_turned()
+            nc.scalar.activation(out=sine_turned[t, cols.start][:], in_=bank[:], func=ACT.Sin, scale=2.0 * math.pi)
 
-        def scale_back(t, cols):
+        def turn_back_and_scale(t, cols):
             bank = take_back_bank()
-            for a in range(0, HW, P):
-                nc.tensor.transpose(bank[:, a : a + P], sine_t[t, cols.start][:, a : a + P], identity[:])
-            nc.scalar.activation(out=x_rows[:, t, cols], in_=bank[:], func=ACT.Copy, scale=gain_sb[:, t : t + 1])
+            for a in range(0, BANK, P):
+                nc.tensor.transpose(bank[:, a : a + P], sine_turned[t, cols.start][:, a : a + P], identity[:])
+            scale_row(t, cols, bank[:])
 
-        def scale_row(t, cols):
-            nc.scalar.activation(out=x_rows[:, t, cols], in_=rest[t][:, cols], func=ACT.Copy, scale=gain_sb[:, t : t + 1])
-
-        def weave(q):
+        def weave_rows(q):
             nc.scalar.copy(
-                out=x_bf[q][:].rearrange("p (j t) -> p j t", t=4)[:, :, 0:3],
-                in_=x_rows[:, :, pieces[q]].rearrange("p t j -> p j t"),
+                out=x_bf[q][:].rearrange("p (j t) -> p j t", t=PACK)[:, :, 0 : PACK - 1],
+                in_=x_rows[:, :, PIECES[q]].rearrange("p t j -> p j t"),
             )
 
-        def scale_last(q):
+        def scale_last_tile(q):
             nc.vector.tensor_scalar(
-                out=x_bf[q][:].rearrange("p (j t) -> p t j", t=4)[:, 3, :], in0=rest[3][:, pieces[q]],
-                scalar1=gain_sb[:, 3:4], scalar2=None, op0=ALU.mult,
+                out=x_bf[q][:].rearrange("p (j t) -> p t j", t=PACK)[:, PACK - 1, :],
+                in0=rest[PACK - 1][:, PIECES[q]],
+                scalar1=gain_sb[:, PACK - 1 : PACK], scalar2=None, op0=ALU.mult,
             )
 
-        take_y_bank = bank_ring(Y_BANKS)
-        take_y = ring("y_sb", Y_RING, [P, HW], F32)
-        spare = [raw[:, j, :] for raw in w1_raw + w3_raw for j in range(4)]
-        stored = []
+        out_rows = out.rearrange("(p t) j -> p t j", t=PACK)
+        take_y = ring("y_sb", PACK, [P, BANK], F32)
+        take_result = in_turn([raw[:, i, :] for raw in w1_raw + w3_raw for i in range(PACK)])
+        y_sums = {}
 
-        def take_result():
-            stored.append(0)
-            return spare[len(stored) - 1]
-
-        sums = {}
-
-        def last_product(q):
-            width = pieces[q].stop - pieces[q].start
-            x_w = kept(f"x_w{q}", [P, width], U32)
-            x_s = kept(f"x_s{q}", [P, width], U8)
-            quantise(x_bf[q][:], x_w[:], x_s[:])
-            for t in range(4):
-                if t * width % HW == 0:
+        def make_y(q):
+            width = PIECES[q].stop - PIECES[q].start
+            codes, plane = quantise(x_bf[q][:], f"x{q}")
+            for t in range(PACK):
+                at = t * width % BANK
+                if at == 0:
                     bank = take_y_bank()
-                sums[q, t] = bank[:, t * width % HW : t * width % HW + width]
+                y_sums[q, t] = bank[:, at : at + width]
                 nc.tensor.matmul_mx(
-                    out=sums[q, t],
-                    lhsT=w4_w[:, 128 * t : 128 * (t + 1)].bitcast(FP8X4),
-                    lhsT_scale=w4_s[:, 128 * t : 128 * (t + 1)],
-                    rhs=x_w[:].bitcast(FP8X4),
-                    rhs_scale=x_s[:],
+                    out=y_sums[q, t],
+                    lhsT=w4_codes[:, P * t : P * (t + 1)].bitcast(FP8X4),
+                    lhsT_scale=w4_plane[:, P * t : P * (t + 1)],
+                    rhs=codes[:].bitcast(FP8X4),
+                    rhs_scale=plane[:],
                     start=True,
                     stop=True,
                 )
 
         def finish(q):
-            cols = pieces[q]
+            cols = PIECES[q]
             width = cols.stop - cols.start
-            rows = HW // width
-            for t in range(4):
-                if t % rows == 0:
+            per_store = BANK // width
+            for t in range(PACK):
+                i = t % per_store
+                if i == 0:
                     result = take_result()
                 y_sb = take_y()
-                nc.scalar.activation(out=y_sb[:, 0:width], in_=sums[q, t], func=ACT.Identity, bias=base_sb[:, t : t + 1])
+                nc.scalar.activation(
+                    out=y_sb[:, 0:width], in_=y_sums[q, t], func=ACT.Identity, bias=base_sb[:, t : t + 1]
+                )
                 nc.vector.tensor_tensor(
-                    out=result[:, t % rows * width : (t % rows + 1) * width],
-                    in0=page[t][:].indirect(list4[:, cols.start // 16 : cols.stop // 16]),
+                    out=result[:, i * width : (i + 1) * width],
+                    in0=page[t][:].indirect(entries(list4, cols)),
                     in1=y_sb[:, 0:width],
                     op=ALU.mult,
                 )
-                if t % rows == rows - 1:
+                if i == per_store - 1:
                     nc.sync.dma_start(
-                        out=out_rows[:, t + 1 - rows : t + 1, cols], in_=result.rearrange("p (i j) -> p i j", i=rows)
+                        out=out_rows[:, t - i : t + 1, cols], in_=result.rearrange("p (i j) -> p i j", i=per_store)
                     )
 
-        last = NCH - 1
-        halves = [slice(0, HW), slice(HW, PN)]
-        quarters = [slice(q * QW, (q + 1) * QW) for q in range(4)]
-        make_h(last, 0)
+        make_h(last, 0, take_h_bank())
         for c in range(last):
-            make_h(c, 1, take_irr())
-        make_h(last, 1)
-        for t in range(4):
+            make_h(c, 1, take_irr_bank())
+        make_h(last, 1, take_h_bank())
+
+        last_tile_chunks = [range(0, 1), range(1, CHUNKS)]
+        for t in range(PACK):
             if t < 2:
-                put_rows(last, t)
-                load_wgs(2, t * 2 * CH, 2 * CH, wgs_tiles[2 + t])
+                put(t, range(last, CHUNKS))
+                load_wgs(2, chunk_pairs[t], wgs_tiles[2 + t])
             elif t == 2:
-                for half in range(2):
-                    put_rows(2 * half, 2, 2)
-                    load_wgs(3, half * 1 * CH, (NCH - 1 if half else 1) * CH, wgs_tiles[2 + half])
-            if t < 3:
-                pick(t)
-                for cols in halves:
+                for n in range(2):
+                    put(2, chunk_pairs[n])
+                    load_wgs(3, last_tile_chunks[n], wgs_tiles[2 + n])
+            if t < PACK - 1:
+                pick_turns(t)
+                for cols in HALVES:
                     round_turns(t, cols)
-                    if t in (0, 1):
-                        negate(t, cols)
-            if t - 1 in (0, 1):
-                scale_back(t - 1, halves[1])
+                    if t in ON_TENSOR:
+                        negate_whole(t, cols)
+            if t - 1 in ON_TENSOR:
+                turn_back_and_scale(t - 1, HALVES[1])
             elif t > 0:
-                reduce(t - 1, slice(0, PN))
-                for cols in halves:
-                    sine(t - 1, cols)
-                for cols in halves:
-                    scale_row(t - 1, cols)
-            if t in (0, 1):
-                for cols in halves:
-                    sine_turned(t, cols)
-                scale_back(t, halves[0])
-        for q in range(len(pieces)):
-            weave(q)
-        put_rows(0, 3, 1)
-        put_rows(1, 3, NCH - 1)
-        deal_w4()
-        pick(3)
-        round_turns(3, quarters[0])
-        round_turns(3, quarters[1])
-        reduce(3, quarters[0])
-        reduce(3, quarters[1])
-        round_turns(3, halves[1])
-        sine(3, quarters[0])
-        scale_last(0)
-        reduce(3, halves[1])
-        last_product(0)
-        sine(3, quarters[1])
-        scale_last(1)
-        last_product(1)
-        sine(3, halves[1])
-        scale_last(2)
-        last_product(2)
-        for q in range(len(pieces)):
+                reduce_on_vector(t - 1, slice(0, PN))
+                for cols in HALVES:
+                    sine_of_rest(t - 1, cols)
+                for cols in HALVES:
+                    scale_row(t - 1, cols, rest[t - 1][:, cols])
+            if t in ON_TENSOR:
+                for cols in HALVES:
+                    sine_on_tensor(t, cols)
+                turn_back_and_scale(t, HALVES[0])
+        for q in range(len(PIECES)):
+            weave_rows(q)
+        for chunks in last_tile_chunks:
+            put(PACK - 1, chunks)
+        deal(w4_codes[:], w4_raw[:])
+        deal(w4_plane[:], w4_plane_raw[:])
+
+        t = PACK - 1
+        pick_turns(t)
+        for cols in PIECES[0:2]:
+            round_turns(t, cols)
+        for cols in PIECES[0:2]:
+            reduce_on_vector(t, cols)
+        round_turns(t, PIECES[2])
+        for q, cols in enumerate(PIECES):
+            sine_of_rest(t, cols)
+            scale_last_tile(q)
+            if q == 0:
+                reduce_on_vector(t, PIECES[2])
+            make_y(q)
+        for q in range(len(PIECES)):
             finish(q)

@@ -32,7 +32,7 @@ HALVES = [slice(0, PN // 2), slice(PN // 2, PN)]
 PIECES = [slice(0, 256), slice(256, 512), slice(512, PN)]
 TABLE_AHEAD = 3
 DAMP_AHEAD = 6
-ON_TENSOR = (0, 1)
+LAST_TILE = PACK - 1
 ROUNDER = 12582912.0
 
 
@@ -105,6 +105,10 @@ def tile_list_fellow_eye_fitting_kernel(
         w2_plane_raw = zeroed_plane("w2_plane_raw", M)
         w4_plane_raw = zeroed_plane("w4_plane_raw", H)
 
+        warm = kept("warm", [P, 4], F32)
+        nc.vector.memset(warm[:, 0:1], 1.0)
+        nc.scalar.activation(out=warm[:, 1:2], in_=warm[:, 0:1], func=ACT.Abs_reciprocal_sqrt)
+
         list1 = load_list("list1", offs)
         w2_rows = kept("w2_rows", [P, M], U8)
         load_scale_rows(w2_rows, w2_scales)
@@ -126,7 +130,7 @@ def tile_list_fellow_eye_fitting_kernel(
         list2 = load_list("list2", offs2)
 
         wgs_rows = wgs.rearrange("(q t) j -> q t j", t=PACK)
-        wgs_tiles = [kept(f"wgs{i}", [P, (3 if i == 3 else 2) * CHUNK], F32) for i in range(4)]
+        wgs_tiles = [kept(f"wgs{i}", [P, 2 * CHUNK], F32) for i in range(4)]
         wgs_held = {}
 
         def load_wgs(t, chunks, tile):
@@ -303,8 +307,8 @@ def tile_list_fellow_eye_fitting_kernel(
         x_bf = [kept(f"x_bf{q}", [P, (cols.stop - cols.start) * PACK], BF16) for q, cols in enumerate(PIECES)]
         take_turns = ring("turns", 2, [P, PN], F32)
         take_whole = ring("whole", 2, [P, PN], U32)
-        rest = {t: kept(f"rest{t}", [P, PN], F32) for t in range(PACK) if t not in ON_TENSOR}
-        x_rows = kept("x_rows", [P, PACK - 1, PN], BF16)
+        rest = kept("rest", [P, PN], F32)
+        x_rows = kept("x_rows", [P, LAST_TILE, PN], BF16)
         identity = kept("identity", [P, P], F32)
         make_identity(nc, identity[:])
         take_minus_whole = ring("minus_whole", 2, [P, BANK], F32)
@@ -325,18 +329,6 @@ def tile_list_fellow_eye_fitting_kernel(
 
         def round_turns(t, cols):
             nc.scalar.activation(out=whole[t][:, cols], in_=turns[t][:, cols], func=ACT.Copy, bias=ROUNDER)
-
-        def reduce_on_vector(t, cols):
-            nc.vector.scalar_tensor_tensor(
-                out=rest[t][:, cols], in0=whole[t][:, cols].bitcast(I32), scalar=ROUNDER, in1=turns[t][:, cols],
-                op0=ALU.subtract, op1=ALU.subtract,
-            )
-
-        def sine_of_rest(t, cols):
-            nc.scalar.activation(out=rest[t][:, cols], in_=rest[t][:, cols], func=ACT.Sin, scale=-2.0 * math.pi)
-
-        def scale_row(t, cols, sine):
-            nc.scalar.activation(out=x_rows[:, t, cols], in_=sine, func=ACT.Copy, scale=gain_sb[:, t : t + 1])
 
         def negate_whole(t, cols):
             minus_whole[t, cols.start] = take_minus_whole()
@@ -360,19 +352,27 @@ def tile_list_fellow_eye_fitting_kernel(
             bank = take_back_bank()
             for a in range(0, BANK, P):
                 nc.tensor.transpose(bank[:, a : a + P], sine_turned[t, cols.start][:, a : a + P], identity[:])
-            scale_row(t, cols, bank[:])
+            nc.scalar.activation(out=x_rows[:, t, cols], in_=bank[:], func=ACT.Copy, scale=gain_sb[:, t : t + 1])
 
         def weave_rows(q):
             nc.scalar.copy(
-                out=x_bf[q][:].rearrange("p (j t) -> p j t", t=PACK)[:, :, 0 : PACK - 1],
+                out=x_bf[q][:].rearrange("p (j t) -> p j t", t=PACK)[:, :, 0:LAST_TILE],
                 in_=x_rows[:, :, PIECES[q]].rearrange("p t j -> p j t"),
             )
 
-        def scale_last_tile(q):
+        def reduce_last_tile(cols):
+            nc.vector.scalar_tensor_tensor(
+                out=rest[:, cols], in0=whole[LAST_TILE][:, cols].bitcast(I32), scalar=ROUNDER,
+                in1=turns[LAST_TILE][:, cols], op0=ALU.subtract, op1=ALU.subtract,
+            )
+
+        def sine_last_tile(q):
+            cols = PIECES[q]
+            nc.scalar.activation(out=rest[:, cols], in_=rest[:, cols], func=ACT.Sin, scale=-2.0 * math.pi)
             nc.vector.tensor_scalar(
-                out=x_bf[q][:].rearrange("p (j t) -> p t j", t=PACK)[:, PACK - 1, :],
-                in0=rest[PACK - 1][:, PIECES[q]],
-                scalar1=gain_sb[:, PACK - 1 : PACK], scalar2=None, op0=ALU.mult,
+                out=x_bf[q][:].rearrange("p (j t) -> p t j", t=PACK)[:, LAST_TILE, :],
+                in0=rest[:, cols],
+                scalar1=gain_sb[:, LAST_TILE:PACK], scalar2=None, op0=ALU.mult,
             )
 
         out_rows = out.rearrange("(p t) j -> p t j", t=PACK)
@@ -426,52 +426,41 @@ def tile_list_fellow_eye_fitting_kernel(
             make_h(c, 1, take_irr_bank())
         make_h(last, 1, take_h_bank())
 
-        last_tile_chunks = [range(0, 1), range(1, CHUNKS)]
-        for t in range(PACK):
+        for t in range(LAST_TILE):
             if t < 2:
                 put(t, range(last, CHUNKS))
                 load_wgs(2, chunk_pairs[t], wgs_tiles[2 + t])
-            elif t == 2:
+            else:
                 for n in range(2):
-                    put(2, chunk_pairs[n])
-                    load_wgs(3, last_tile_chunks[n], wgs_tiles[2 + n])
-            if t < PACK - 1:
-                pick_turns(t)
-                for cols in HALVES:
-                    round_turns(t, cols)
-                    if t in ON_TENSOR:
-                        negate_whole(t, cols)
-            if t - 1 in ON_TENSOR:
+                    put(t, chunk_pairs[n])
+                    load_wgs(LAST_TILE, chunk_pairs[n], wgs_tiles[2 + n])
+            pick_turns(t)
+            for cols in HALVES:
+                round_turns(t, cols)
+                negate_whole(t, cols)
+            if t > 0:
                 turn_back_and_scale(t - 1, HALVES[1])
-            elif t > 0:
-                reduce_on_vector(t - 1, slice(0, PN))
-                for cols in HALVES:
-                    sine_of_rest(t - 1, cols)
-                for cols in HALVES:
-                    scale_row(t - 1, cols, rest[t - 1][:, cols])
-            if t in ON_TENSOR:
-                for cols in HALVES:
-                    sine_on_tensor(t, cols)
-                turn_back_and_scale(t, HALVES[0])
+            for cols in HALVES:
+                sine_on_tensor(t, cols)
+            turn_back_and_scale(t, HALVES[0])
+        turn_back_and_scale(LAST_TILE - 1, HALVES[1])
         for q in range(len(PIECES)):
             weave_rows(q)
-        for chunks in last_tile_chunks:
-            put(PACK - 1, chunks)
+        for chunks in chunk_pairs:
+            put(LAST_TILE, chunks)
         deal(w4_codes[:], w4_raw[:])
         deal(w4_plane[:], w4_plane_raw[:])
 
-        t = PACK - 1
-        pick_turns(t)
+        pick_turns(LAST_TILE)
         for cols in PIECES[0:2]:
-            round_turns(t, cols)
+            round_turns(LAST_TILE, cols)
         for cols in PIECES[0:2]:
-            reduce_on_vector(t, cols)
-        round_turns(t, PIECES[2])
-        for q, cols in enumerate(PIECES):
-            sine_of_rest(t, cols)
-            scale_last_tile(q)
+            reduce_last_tile(cols)
+        round_turns(LAST_TILE, PIECES[2])
+        for q in range(len(PIECES)):
+            sine_last_tile(q)
             if q == 0:
-                reduce_on_vector(t, PIECES[2])
+                reduce_last_tile(PIECES[2])
             make_y(q)
         for q in range(len(PIECES)):
             finish(q)

import math
from contextlib import ExitStack

import concourse.mybir as mybir
from concourse.masks import make_identity

K, M, H = 512, 1024, 512
T, T2 = 2048, 2048
S, PN = 1024, 1024
FLOPS = 2 * (2 * K * M * S + M * H * S + H * H * PN)

F32 = mybir.dt.float32
BF16 = mybir.dt.bfloat16
I32 = mybir.dt.int32
U32 = mybir.dt.uint32
U16 = mybir.dt.uint16
U8 = mybir.dt.uint8
FP8X4 = mybir.dt.float8_e4m3fn_x4
FP4X4 = mybir.dt.float4_e2m1fn_x4
ALU = mybir.AluOpType
ACT = mybir.ActivationFunctionType

P = 128
PACK = 4
PASS = P * PACK
BANK = 512
STRIPE = 16
CHUNK = 256
CHUNKS = S // CHUNK
UNIT = BANK // PACK
HALVES = [slice(0, PN // 2), slice(PN // 2, PN)]
PIECES = [slice(0, 256), slice(256, 512), slice(512, PN)]
TABLE_AHEAD = 3
DAMP_AHEAD = 6
LAST_TILE = PACK - 1
ROUNDER = 12582912.0


def tile_list_fellow_eye_fitting_kernel(
    tc, tab_words, tab_scales, w1, w2_words, w2_scales, w3, wgs, page0, gain,
    w4_words, w4_scales, base, offs, offs2, offs3, offs4, out,
):
    nc = tc.nc
    with ExitStack() as ctx:
        lists = ctx.enter_context(tc.tile_pool(name="lists", bufs=1))
        keep = ctx.enter_context(tc.tile_pool(name="keep", bufs=1))
        psum = ctx.enter_context(tc.psum_pool(name="psum", bufs=1))

        def kept(name, shape, dtype):
            return keep.tile(shape, dtype, name=name, align_bytes=64)

        def in_turn(members):
            taken = []

            def take():
                taken.append(None)
                return members[(len(taken) - 1) % len(members)]

            return take

        def ring(name, count, shape, dtype):
            return in_turn([kept(f"{name}{i}", shape, dtype) for i in range(count)])

        def entries(list_tile, cols):
            return list_tile[:, cols.start // STRIPE : cols.stop // STRIPE]

        def quantise(values_bf, name):
            width = values_bf.shape[1] // PACK
            codes = kept(name + "_codes", [P, width], U32)
            plane = kept(name + "_plane", [P, width], U8)
            nc.vector.quantize_mx(out=codes[:].bitcast(FP8X4), scales=plane[:], in_=values_bf)
            return codes, plane

        banks = [psum.tile([P, BANK], F32, name=f"bank{i}") for i in range(8)]
        take_irr_bank = in_turn(banks[0:3])
        take_curv_bank = in_turn([banks[3], banks[4], banks[7]])
        take_h_bank = in_turn(banks[5:7])
        take_turned_bank = in_turn(banks[3:5])
        take_back_bank = in_turn([banks[7], banks[0]])
        take_y_bank = in_turn(banks)

        def load_list(name, src):
            tile = lists.tile([P, src.shape[1]], U16, name=name)
            nc.sync.dma_start(tile[:], src)
            return tile

        def zeroed_plane(name, width):
            plane = kept(name, [P, width], U8)
            nc.vector.memset(plane[:].bitcast(I32), 0)
            return plane

        def load_scale_rows(plane, src):
            for quad in range(4):
                nc.sync.dma_start(
                    out=plane[32 * quad : 32 * quad + 4, :].bitcast(I32),
                    in_=src[0, 4 * quad : 4 * quad + 4, :].bitcast(I32),
                )

        def load_column(name, vec):
            tile = kept(name, [P, PACK], F32)
            nc.sync.dma_start(out=tile[:], in_=vec.rearrange("(p t) -> p t", t=PACK))
            return tile

        tab_plane = zeroed_plane("tab_plane", T)
        w2_plane_raw = zeroed_plane("w2_plane_raw", M)
        w4_plane_raw = zeroed_plane("w4_plane_raw", H)

        warm = kept("warm", [P, 4], F32)
        nc.vector.memset(warm[:, 0:1], 1.0)
        nc.scalar.activation(out=warm[:, 1:2], in_=warm[:, 0:1], func=ACT.Abs_reciprocal_sqrt)

        list1 = load_list("list1", offs)
        w2_rows = kept("w2_rows", [P, M], U8)
        load_scale_rows(w2_rows, w2_scales)
        w2_raw = kept("w2_raw", [P, M // 2], I32)
        nc.sync.dma_start(out=w2_raw[:], in_=w2_words[0].bitcast(I32))
        tab_codes = kept("tab_codes", [P, T], I32)
        nc.sync.dma_start(out=tab_codes[:], in_=tab_words[0].rearrange("p t i -> p (t i)").bitcast(I32))
        load_scale_rows(tab_plane, tab_scales)
        w1_raw = [kept(f"w1_raw{b}", [P, PACK, PASS], F32) for b in range(2)]
        w3_raw = [kept(f"w3_raw{b}", [P, PACK, H], F32) for b in range(2)]
        for b in range(2):
            nc.sync.dma_start(
                out=w1_raw[b][:], in_=w1[:, PASS * b : PASS * (b + 1)].rearrange("(p i) m -> p i m", i=PACK)
            )
        for b in range(2):
            nc.sync.dma_start(
                out=w3_raw[b][:], in_=w3[PASS * b : PASS * (b + 1), :].rearrange("(p i) r -> p i r", i=PACK)
            )
        list2 = load_list("list2", offs2)

        wgs_rows = wgs.rearrange("(q t) j -> q t j", t=PACK)
        wgs_tiles = [kept(f"wgs{i}", [P, 2 * CHUNK], F32) for i in range(4)]
        wgs_held = {}

        def load_wgs(t, chunks, tile):
            for c in chunks:
                wgs_held[t, c] = (tile, (c - chunks.start) * CHUNK)
            for quad in range(4):
                nc.sync.dma_start(
                    out=tile[32 * quad : 32 * (quad + 1), 0 : len(chunks) * CHUNK],
                    in_=wgs_rows[:, t, chunks.start * CHUNK : chunks.stop * CHUNK],
                )

        page_rows = page0.rearrange("(p t) c -> p t c", t=PACK)
        page = [kept(f"page{t}", [P, T2], F32) for t in range(PACK)]
        chunk_pairs = [range(0, 2), range(2, 4)]
        for t in range(2):
            load_wgs(t, chunk_pairs[0], wgs_tiles[t])
            nc.sync.dma_start(out=page[t][:], in_=page_rows[:, t, :])
        for t in range(2):
            load_wgs(t, chunk_pairs[1], wgs_tiles[2 + t])
        w4_raw = kept("w4_raw", [P, H], I32)
        nc.sync.dma_start(out=w4_raw[:], in_=w4_words[0].rearrange("p c i -> p (c i)").bitcast(I32))
        load_scale_rows(w4_plane_raw, w4_scales)
        list3 = load_list("list3", offs3)
        gain_sb = load_column("gain_sb", gain)
        for t in range(2, PACK):
            nc.sync.dma_start(out=page[t][:], in_=page_rows[:, t, :])
        list4 = load_list("list4", offs4)
        base_sb = load_column("base_sb", base)

        def deal(dst, src):
            nc.vector.tensor_copy(
                out=dst.rearrange("p (t q) -> p q t", t=PACK), in_=src.rearrange("p (q t) -> p q t", t=PACK)
            )

        w2_codes = kept("w2_codes", [P, 2 * M], U8)
        w2_plane = kept("w2_plane", [P, M], U8)
        for quad in range(4):
            live = slice(32 * quad, 32 * quad + 4)
            nc.vector.tensor_copy(out=w2_plane_raw[live, :].bitcast(I32), in_=w2_rows[live, :].bitcast(I32))
        for b in range(2):
            cols = slice(PASS * b, PASS * (b + 1))
            deal(w2_plane[:, cols], w2_plane_raw[:, cols])
            deal(w2_codes[:].bitcast(U16)[:, cols], w2_raw[:].bitcast(U16)[:, cols])

        take_v_codes = ring("v_codes", TABLE_AHEAD, [P, CHUNK], U32)
        take_v_plane = ring("v_plane", TABLE_AHEAD, [P, CHUNK], U8)
        v_codes = {}
        v_plane = {}

        def gather_table(c):
            v_codes[c] = take_v_codes()
            v_plane[c] = take_v_plane()
            picks = entries(list1, slice(c * CHUNK, (c + 1) * CHUNK))
            nc.vector.tensor_copy(out=v_codes[c][:], in_=tab_codes[:].bitcast(U32).indirect(picks))
            nc.vector.tensor_copy(out=v_plane[c][:], in_=tab_plane[:].indirect(picks))

        take_weight_bf = ring("weight_bf", 2, [P, PASS * PACK], BF16)

        def quantise_weight(name, raw):
            weight_bf = take_weight_bf()
            nc.vector.tensor_copy(
                out=weight_bf[:].rearrange("p (t q i) -> p q i t", t=PACK, i=PACK),
                in_=raw[:].rearrange("p i (q t) -> p q i t", t=PACK),
            )
            return quantise(weight_bf[:], name)

        take_damp = ring("damp", DAMP_AHEAD, [P, BANK], F32)
        take_ratio_bf = ring("ratio_bf", 2, [P, 2 * CHUNK * PACK], BF16)
        w1_q = {}
        w3_q = {}
        ratio_bf = {}
        ratio_q = {}

        def row_tiles(bank, weight_codes, weight_plane, c, cols):
            for t in range(PACK):
                nc.tensor.matmul_mx(
                    out=bank[:, UNIT * t : UNIT * (t + 1)],
                    lhsT=weight_codes(t),
                    lhsT_scale=weight_plane[:, P * t : P * (t + 1)],
                    rhs=v_codes[c][:, cols].bitcast(FP8X4),
                    rhs_scale=v_plane[c][:, cols],
                    start=True,
                    stop=True,
                )

        def ratio_pass(c, b):
            units = [slice(first, first + UNIT) for first in range(0, CHUNK, UNIT)]
            damps = []
            for cols in units:
                irr = take_irr_bank()
                row_tiles(
                    irr,
                    lambda t: w2_codes[:, 2 * (PASS * b + P * t) : 2 * (PASS * b + P * (t + 1))].bitcast(FP4X4),
                    w2_plane[:, PASS * b : PASS * (b + 1)],
                    c,
                    cols,
                )
                damp = take_damp()
                nc.scalar.activation(
                    out=damp[:].rearrange("p (j t) -> p j t", t=PACK),
                    in_=irr[:].rearrange("p (t j) -> p j t", t=PACK),
                    func=ACT.Abs,
                )
                damps.append(damp)
            for damp in damps:
                nc.scalar.activation(out=damp[:], in_=damp[:], func=ACT.Abs_reciprocal_sqrt, bias=1.0)
            for damp in damps:
                nc.scalar.activation(out=damp[:], in_=damp[:], func=ACT.Square)
            if b == 0:
                ratio_bf[c] = take_ratio_bf()
            for cols, damp in zip(units, damps):
                curv = take_curv_bank()
                row_tiles(curv, lambda t: w1_q[b][0][:, P * t : P * (t + 1)].bitcast(FP8X4), w1_q[b][1], c, cols)
                words = slice((b * CHUNK + cols.start) * PACK, (b * CHUNK + cols.stop) * PACK)
                nc.vector.tensor_tensor(
                    out=ratio_bf[c][:, words].rearrange("p (j t) -> p j t", t=PACK),
                    in0=curv[:].rearrange("p (t j) -> p j t", t=PACK),
                    in1=damp[:].rearrange("p (j t) -> p j t", t=PACK),
                    op=ALU.mult,
                )
            if b == 1:
                ratio_q[c] = quantise(ratio_bf[c][:], f"ratio{c}")

        h_sb = [kept(f"h{pair}", [P, 2, S], F32) for pair in range(2)]

        def make_h(c, pair, bank):
            codes, plane = ratio_q[c]
            for i in range(2):
                t = 2 * pair + i
                for b in range(2):
                    nc.tensor.matmul_mx(
                        out=bank[:, CHUNK * i : CHUNK * (i + 1)],
                        lhsT=w3_q[b][0][:, P * t : P * (t + 1)].bitcast(FP8X4),
                        lhsT_scale=w3_q[b][1][:, P * t : P * (t + 1)],
                        rhs=codes[:, b * CHUNK : (b + 1) * CHUNK].bitcast(FP8X4),
                        rhs_scale=plane[:, b * CHUNK : (b + 1) * CHUNK],
                        start=(b == 0),
                        stop=(b == 1),
                    )
            nc.scalar.copy(
                out=h_sb[pair][:, :, c * CHUNK : (c + 1) * CHUNK], in_=bank[:].rearrange("p (i j) -> p i j", i=2)
            )

        def put(t, chunks):
            cols = slice(chunks.start * CHUNK, chunks.stop * CHUNK)
            wgs_tile, at = wgs_held[t, chunks.start]
            nc.vector.tensor_tensor(
                out=page[t][:].indirect(entries(list2, cols)),
                in0=h_sb[t // 2][:, t % 2, cols],
                in1=wgs_tile[:, at : at + len(chunks) * CHUNK],
                op=ALU.mult,
            )

        gather_table(0)
        w1_q[0] = quantise_weight("w1_0", w1_raw[0])
        ratio_pass(0, 0)
        w1_q[1] = quantise_weight("w1_1", w1_raw[1])
        gather_table(1)
        ratio_pass(0, 1)
        for b in range(2):
            w3_q[b] = quantise_weight(f"w3_{b}", w3_raw[b])
        last = CHUNKS - 1
        for c in range(last):
            if c + 2 < CHUNKS:
                gather_table(c + 2)
            ratio_pass(c + 1, 0)
            ratio_pass(c + 1, 1)
            make_h(c, 0, take_h_bank())
            for t in range(2):
                put(t, range(c, c + 1))

        w4_codes = kept("w4_codes", [P, H], I32)
        w4_plane = kept("w4_plane", [P, H], U8)
        x_bf = [kept(f"x_bf{q}", [P, (cols.stop - cols.start) * PACK], BF16) for q, cols in enumerate(PIECES)]
        take_turns = ring("turns", 2, [P, PN], F32)
        take_whole = ring("whole", 2, [P, PN], U32)
        rest = kept("rest", [P, PN], F32)
        x_rows = kept("x_rows", [P, LAST_TILE, PN], BF16)
        identity = kept("identity", [P, P], F32)
        make_identity(nc, identity[:])
        take_minus_whole = ring("minus_whole", 2, [P, BANK], F32)
        take_sine_turned = ring("sine_turned", 2, [P, BANK], F32)
        turns = {}
        whole = {}
        minus_whole = {}
        sine_turned = {}

        def pick_turns(t):
            turns[t] = take_turns()
            whole[t] = take_whole()
            for cols in HALVES:
                nc.vector.tensor_scalar(
                    out=turns[t][:, cols], in0=page[t][:].indirect(entries(list3, cols)),
                    scalar1=1.0 / (2.0 * math.pi), scalar2=0.0, op0=ALU.mult, op1=ALU.add,
                )

        def round_turns(t, cols):
            nc.scalar.activation(out=whole[t][:, cols], in_=turns[t][:, cols], func=ACT.Copy, bias=ROUNDER)

        def negate_whole(t, cols):
            minus_whole[t, cols.start] = take_minus_whole()
            nc.scalar.activation(
                out=minus_whole[t, cols.start][:], in_=whole[t][:, cols], func=ACT.Copy, scale=-1.0, bias=ROUNDER
            )

        def sine_on_tensor(t, cols):
            bank = take_turned_bank()
            terms = [turns[t][:, cols], minus_whole[t, cols.start][:]]
            for n, term in enumerate(terms):
                for a in range(0, BANK, P):
                    nc.tensor.matmul(
                        out=bank[:, a : a + P], lhsT=term[:, a : a + P], rhs=identity[:],
                        start=(n == 0 and a == 0), stop=(n == 1 and a == BANK - P), is_transpose=True,
                    )
            sine_turned[t, cols.start] = take_sine_turned()
            nc.scalar.activation(out=sine_turned[t, cols.start][:], in_=bank[:], func=ACT.Sin, scale=2.0 * math.pi)

        def turn_back_and_scale(t, cols):
            bank = take_back_bank()
            for a in range(0, BANK, P):
                nc.tensor.transpose(bank[:, a : a + P], sine_turned[t, cols.start][:, a : a + P], identity[:])
            nc.scalar.activation(out=x_rows[:, t, cols], in_=bank[:], func=ACT.Copy, scale=gain_sb[:, t : t + 1])

        def weave_rows(q):
            nc.scalar.copy(
                out=x_bf[q][:].rearrange("p (j t) -> p j t", t=PACK)[:, :, 0:LAST_TILE],
                in_=x_rows[:, :, PIECES[q]].rearrange("p t j -> p j t"),
            )

        def reduce_last_tile(cols):
            nc.vector.scalar_tensor_tensor(
                out=rest[:, cols], in0=whole[LAST_TILE][:, cols].bitcast(I32), scalar=ROUNDER,
                in1=turns[LAST_TILE][:, cols], op0=ALU.subtract, op1=ALU.subtract,
            )

        def sine_last_tile(q):
            cols = PIECES[q]
            nc.scalar.activation(out=rest[:, cols], in_=rest[:, cols], func=ACT.Sin, scale=-2.0 * math.pi)
            nc.vector.tensor_scalar(
                out=x_bf[q][:].rearrange("p (j t) -> p t j", t=PACK)[:, LAST_TILE, :],
                in0=rest[:, cols],
                scalar1=gain_sb[:, LAST_TILE:PACK], scalar2=None, op0=ALU.mult,
            )

        out_rows = out.rearrange("(p t) j -> p t j", t=PACK)
        take_y = ring("y_sb", PACK, [P, BANK], F32)
        take_result = in_turn([raw[:, i, :] for raw in w1_raw + w3_raw for i in range(PACK)])
        y_sums = {}

        def make_y(q):
            width = PIECES[q].stop - PIECES[q].start
            codes, plane = quantise(x_bf[q][:], f"x{q}")
            for t in range(PACK):
                at = t * width % BANK
                if at == 0:
                    bank = take_y_bank()
                y_sums[q, t] = bank[:, at : at + width]
                nc.tensor.matmul_mx(
                    out=y_sums[q, t],
                    lhsT=w4_codes[:, P * t : P * (t + 1)].bitcast(FP8X4),
                    lhsT_scale=w4_plane[:, P * t : P * (t + 1)],
                    rhs=codes[:].bitcast(FP8X4),
                    rhs_scale=plane[:],
                    start=True,
                    stop=True,
                )

        def finish(q):
            cols = PIECES[q]
            width = cols.stop - cols.start
            per_store = BANK // width
            for t in range(PACK):
                i = t % per_store
                if i == 0:
                    result = take_result()
                y_sb = take_y()
                nc.scalar.activation(
                    out=y_sb[:, 0:width], in_=y_sums[q, t], func=ACT.Identity, bias=base_sb[:, t : t + 1]
                )
                nc.vector.tensor_tensor(
                    out=result[:, i * width : (i + 1) * width],
                    in0=page[t][:].indirect(entries(list4, cols)),
                    in1=y_sb[:, 0:width],
                    op=ALU.mult,
                )
                if i == per_store - 1:
                    nc.sync.dma_start(
                        out=out_rows[:, t - i : t + 1, cols], in_=result.rearrange("p (i j) -> p i j", i=per_store)
                    )

        make_h(last, 0, take_h_bank())
        for c in range(last):
            make_h(c, 1, take_irr_bank())
        make_h(last, 1, take_h_bank())

        for t in range(LAST_TILE):
            if t < 2:
                put(t, range(last, CHUNKS))
                load_wgs(2, chunk_pairs[t], wgs_tiles[2 + t])
            else:
                for n in range(2):
                    put(t, chunk_pairs[n])
                    load_wgs(LAST_TILE, chunk_pairs[n], wgs_tiles[2 + n])
            pick_turns(t)
            for cols in HALVES:
                round_turns(t, cols)
                negate_whole(t, cols)
            if t > 0:
                turn_back_and_scale(t - 1, HALVES[1])
            for cols in HALVES:
                sine_on_tensor(t, cols)
            turn_back_and_scale(t, HALVES[0])
        turn_back_and_scale(LAST_TILE - 1, HALVES[1])
        for q in range(len(PIECES)):
            weave_rows(q)
        for chunks in chunk_pairs:
            put(LAST_TILE, chunks)
        deal(w4_codes[:], w4_raw[:])
        deal(w4_plane[:], w4_plane_raw[:])

        pick_turns(LAST_TILE)
        for cols in PIECES[0:2]:
            round_turns(LAST_TILE, cols)
        for cols in PIECES[0:2]:
            reduce_last_tile(cols)
        round_turns(LAST_TILE, PIECES[2])
        for q in range(len(PIECES)):
            sine_last_tile(q)
            if q == 0:
                reduce_last_tile(PIECES[2])
            make_y(q)
        for q in range(len(PIECES)):
            finish(q)
